import numpy as np
import ml_dtypes


def mxq(x, axis, fmt="e4m3"):
    dtype, down = {"e4m3": (ml_dtypes.float8_e4m3fn, 7), "e5m2": (ml_dtypes.float8_e5m2, 14)}[fmt]
    v = np.moveaxis(np.asarray(x, np.float32).astype(ml_dtypes.bfloat16).astype(np.float64), axis, -1)
    blocks = v.reshape(v.shape[:-1] + (-1, 32))
    amax = np.abs(blocks).max(-1, keepdims=True)
    byte = np.maximum(np.where(amax > 0, np.frexp(amax)[1] - 1 + 127, 0) - down, 1)
    scale = np.exp2(byte - 127.0)
    codes = (blocks / scale).astype(np.float32).astype(dtype).astype(np.float64)
    return np.moveaxis((codes * scale).reshape(v.shape), -1, axis)


WIDE = False


def mx_kscale(k):
    if not WIDE:
        return np.ones(k)
    levels = np.array([24, -24, 12, -12, 0])
    if k % 512:
        return np.exp2(np.random.permutation(np.resize(levels, k // 32))).repeat(32)
    a = np.empty((k // 512, 16))
    for p in range(k // 512):
        a[p, :8] = np.random.permutation(np.resize(levels, 8))
        for g in range(8):
            far = levels[np.abs(levels - a[p, g]) >= 10]
            a[p, g + 8] = far[np.random.randint(len(far))]
    return np.exp2(a.ravel()).repeat(32)


def f64(x):
    return np.asarray(x).astype(np.float64)


def striped8(idx):
    return np.concatenate([v.reshape(-1, 16).T for v in idx]).astype(np.uint16)


def unstriped8(offs):
    return np.stack([offs[16 * g:16 * g + 16].T.reshape(-1) for g in range(8)]).astype(np.int64)


E2M1 = np.array([0.0, 0.5, 1.0, 1.5, 2.0, 3.0, 4.0, 6.0, -0.0, -0.5, -1.0, -1.5, -2.0, -3.0, -4.0, -6.0])


def pack_weight(w, fmt):
    k, n = w.shape
    w = f64(np.asarray(w, np.float32).astype(ml_dtypes.bfloat16)).reshape(k // 32, 32, n)
    amax = np.abs(w).max(1)
    if fmt == "e4m3":
        byte = np.frexp(amax)[1] - 1 + 127 - 7
    else:
        mant, ex = np.frexp(amax / 6.0)
        byte = np.where(mant > 0.5, ex, ex - 1) + 127
    byte = np.clip(np.where(amax > 0, byte, 1), 1, 254)
    scaled = (w * np.exp2(127.0 - byte)[:, None, :]).reshape(k, n).astype(np.float32)
    by_word = np.ascontiguousarray(scaled.reshape(k // 512, 128, 4, n).transpose(0, 1, 3, 2))
    if fmt == "e4m3":
        words = by_word.astype(ml_dtypes.float8_e4m3fn).view(np.uint8)
    else:
        c = by_word.astype(ml_dtypes.float4_e2m1fn).view(np.uint8) & 0xF
        words = (c[..., 0::2] | (c[..., 1::2] << 4)).reshape(k // 512, 128, 2 * n)
    return np.ascontiguousarray(words), np.ascontiguousarray(byte.astype(np.uint8).reshape(k // 512, 16, n))


def unpack_weight(words, scales, fmt):
    g, _, n = scales.shape
    words = np.ascontiguousarray(words).reshape(g, 128, n, -1)
    if fmt == "e4m3":
        vals = words.view(ml_dtypes.float8_e4m3fn).astype(np.float64)
    else:
        nib = np.empty((g, 128, n, 4), np.uint8)
        nib[..., 0::2] = words & 0xF
        nib[..., 1::2] = words >> 4
        vals = E2M1[nib]
    vals = vals * np.repeat(np.exp2(scales.astype(np.float64) - 127.0), 8, axis=1)[..., None]
    return vals.transpose(0, 1, 3, 2).reshape(g * 512, n)


K, L, N, T, J = 1024, 512, 512, 2048, 1024


def setup_inputs():
    n = np.random.standard_normal
    s = mx_kscale(K)[:, None]
    s2 = mx_kscale(L)[:, None]
    p_wt = pack_weight(n((K, N)) / np.sqrt(K) / s, "e4m3")
    p_wx = pack_weight(n((L, N)) / np.sqrt(L) / s2, "e4m3")
    return {
        "xT": (n((K, T)) * s).astype(np.float32),
        "wgt": np.repeat(np.random.uniform(0.5, 2.0, (8, J)), 16, axis=0).astype(np.float32),
        "wt_words": p_wt[0],
        "wt_scales": p_wt[1],
        "c": (n((L, J)) * s2).astype(np.float32),
        "wx_words": p_wx[0],
        "wx_scales": p_wx[1],
        "b": (0.3 * n(N)).astype(np.float32),
        "wgo": np.repeat(np.random.uniform(0.5, 2.0, (8, J)), 16, axis=0).astype(np.float32),
        "offs": striped8(np.stack([np.random.permutation(T)[:J] for _ in range(8)])),
        "offs2": striped8(np.stack([np.random.permutation(T)[:J] for _ in range(8)])),
    }


def reference(xT, wgt, wt_words, wt_scales, c, wx_words, wx_scales, b, wgo, offs, offs2):
    idx = unstriped8(offs)
    idx2 = unstriped8(offs2)
    rows = np.arange(K)
    xg = f64(wgt)[rows // 4 % 128] * f64(xT)[rows[:, None], idx[rows % 512 // 64]]
    xT_ = mxq(xg, 0, "e4m3")
    wt_ = unpack_weight(wt_words, wt_scales, "e4m3")
    c_q_ = mxq(f64(c), 0, "e4m3")
    c_r_ = mxq(f64(c) - c_q_, 0, "e4m3")
    wx_ = unpack_weight(wx_words, wx_scales, "e4m3")
    y = wt_.T @ xT_ + wx_.T @ c_q_ + wx_.T @ c_r_
    out = np.zeros((N, T))
    rows = np.arange(N)
    out[rows[:, None], idx2[rows % 128 // 16]] = f64(wgo)[rows % 128] * (y + f64(b)[:, None])
    return out

@@ -1,0 +1,264 @@
+from contextlib import ExitStack
+
+import concourse.mybir as mybir
+from concourse.masks import make_identity
+
+K, L, N, T, J = 1024, 512, 512, 2048, 1024
+FLOPS = 2 * (K + 2 * L) * N * J + 2 * L * L * J
+
+F32 = mybir.dt.float32
+BF16 = mybir.dt.bfloat16
+I32 = mybir.dt.int32
+U32 = mybir.dt.uint32
+U16 = mybir.dt.uint16
+U8 = mybir.dt.uint8
+FP8X4 = mybir.dt.float8_e4m3fn_x4
+MULT = mybir.AluOpType.mult
+SUB = mybir.AluOpType.subtract
+IDENT = mybir.ActivationFunctionType.Identity
+
+P = 128
+PACK = 4
+HALF = J // 2
+CH = 256
+DQ = 128
+
+
+def tile_list_scatb_kernel(
+    tc, xT, wgt, wt_words, wt_scales, c, wx_words, wx_scales, b, wgo, offs, offs2, out
+):
+    nc = tc.nc
+    with ExitStack() as ctx:
+        keep = ctx.enter_context(tc.tile_pool(name="keep", bufs=1))
+        ring = ctx.enter_context(tc.tile_pool(name="ring", bufs=3))
+        psum = ctx.enter_context(tc.psum_pool(name="psum", bufs=1))
+
+        offs_sb = keep.tile([P, J // 16], U16, name="offs_sb")
+        offs2_sb = keep.tile([P, J // 16], U16, name="offs2_sb")
+        x_sb = [keep.tile([P, T], F32, name="x%d" % q) for q in range(8)]
+        wgt_sb = [keep.tile([P, HALF], F32, name="wgt%d" % h) for h in range(2)]
+        wgo_sb = [keep.tile([P, HALF], F32, name="wgo%d" % h) for h in range(2)]
+        c_sb = [keep.tile([P, PACK, CH], F32, name="c%d" % u) for u in range(4)]
+        wt_w = keep.tile([P, 2, N], U32, name="wt_w", align_bytes=64)
+        wx_w = keep.tile([P, N], U32, name="wx_w", align_bytes=64)
+        w_s = keep.tile([P, 3, N], U8, name="w_s", align_bytes=64)
+        bias = keep.tile([P, N // P], F32, name="bias")
+        eye = keep.tile([P, P], BF16, name="eye")
+        eye4 = keep.tile([P, PACK * (L + 1)], BF16, name="eye4", align_bytes=64)
+        eye_w = keep.tile([P, L], U32, name="eye_w", align_bytes=64)
+        eye_s = keep.tile([P, L], U8, name="eye_s", align_bytes=64)
+        act_w = [[keep.tile([P, HALF], U32, name="aw%d%d" % (h, o), align_bytes=64) for o in range(4)] for h in range(2)]
+        act_s = [[keep.tile([P, HALF], U8, name="as%d%d" % (h, o), align_bytes=64) for o in range(4)] for h in range(2)]
+        win = [keep.tile([P, T], F32, name="win%d" % w) for w in range(3)]
+        gath = [[keep.tile([P, PACK, HALF], F32, name="g%d%d" % (a, h)) for h in range(2)] for a in range(2)]
+
+        x_planes = xT.rearrange("(a p i) t -> a i p t", a=2, i=PACK)
+        c_rows = c.rearrange("(p i) j -> p i j", i=PACK)
+
+        def load_x(q):
+            nc.sync.dma_start(out=x_sb[q][:], in_=x_planes[q // PACK, q % PACK])
+
+        def load_c(u):
+            nc.sync.dma_start(out=c_sb[u][:], in_=c_rows[:, :, u * CH:(u + 1) * CH])
+
+        def load_half(tile, src, h):
+            nc.sync.dma_start(out=tile[h][:], in_=src[:, h * HALF:(h + 1) * HALF])
+
+        def load_scales(q):
+            nc.sync.dma_start(
+                out=w_s[32 * q:32 * q + 4, 0:2, :].bitcast(I32),
+                in_=wt_scales[:, 4 * q:4 * q + 4, :].rearrange("a r n -> r a n").bitcast(I32),
+            )
+            nc.sync.dma_start(
+                out=w_s[32 * q:32 * q + 4, 2, :].bitcast(I32),
+                in_=wx_scales[0, 4 * q:4 * q + 4, :].bitcast(I32),
+            )
+
+        nc.vector.memset(w_s[:].rearrange("p a n -> p (a n)").bitcast(I32), 0)
+        nc.sync.dma_start(offs_sb[:], offs)
+        load_half(wgt_sb, wgt, 0)
+        load_x(0)
+        load_half(wgt_sb, wgt, 1)
+        load_c(0)
+        load_x(1)
+        load_c(1)
+        load_x(2)
+        load_c(2)
+        load_x(3)
+        load_c(3)
+        load_x(4)
+        load_x(5)
+        load_scales(0)
+        load_scales(1)
+        load_x(6)
+        load_scales(2)
+        load_scales(3)
+        load_x(7)
+        nc.sync.dma_start(out=wx_w[:].bitcast(I32), in_=wx_words[0].rearrange("p n i -> p (n i)").bitcast(I32))
+        nc.sync.dma_start(out=wt_w[:].bitcast(I32), in_=wt_words.rearrange("a p n i -> p a (n i)").bitcast(I32))
+        nc.sync.dma_start(offs2_sb[:], offs2)
+        load_half(wgo_sb, wgo, 0)
+        with nc.allow_non_contiguous_dma(reason="one bias value to a partition and output tile"):
+            nc.sync.dma_start(out=bias[:], in_=b.rearrange("(m p) -> p m", p=P))
+        load_half(wgo_sb, wgo, 1)
+
+        make_identity(nc, eye[:])
+
+        nc.vector.memset(eye4[:].bitcast(I32), 0)
+        nc.scalar.copy(
+            out=eye4[:].rearrange("p (t x) -> p t x", t=PACK)[:, :, 0:L:PACK],
+            in_=eye[:].unsqueeze(1).to_broadcast([P, PACK, P]),
+        )
+        nc.vector.memset(win[0][:], 0.0)
+        nc.vector.memset(win[1][:], 0.0)
+        nc.vector.memset(win[2][:], 0.0)
+        nc.vector.quantize_mx(out=eye_w[:].bitcast(FP8X4), scales=eye_s[:], in_=eye4[:, 0:PACK * L])
+
+        def by_fours_src(ap):
+            return ap.rearrange("p t (g e) -> p g t e", e=4)
+
+        def by_fours_dst(ap):
+            return ap.rearrange("p (g e t) -> p g t e", e=4, t=PACK)
+
+        def interleave(src):
+            z = ring.tile([P, PACK * CH], BF16, name="z", tag="z", bufs=6, align_bytes=64)
+            nc.scalar.copy(out=by_fours_dst(z[:]), in_=by_fours_src(src))
+            return z
+
+        def quantise(z, h, o, j0):
+            nc.vector.quantize_mx(
+                out=act_w[h][o][:, j0:j0 + CH].bitcast(FP8X4), scales=act_s[h][o][:, j0:j0 + CH], in_=z[:]
+            )
+
+        resid = {}
+
+        def tier_one(u):
+            quantise(interleave(c_sb[u][:]), u // 2, 2, (u % 2) * CH)
+
+        def residual(u):
+            h, j0 = u // 2, (u % 2) * CH
+            r = ring.tile([P, PACK * CH], BF16, name="r", tag="r", bufs=2, align_bytes=64)
+            for s in range(CH // DQ):
+                dq = psum.tile([P, PACK, DQ], F32, name="dq", tag="dq", bufs=3)
+                cols = slice(j0 + s * DQ, j0 + (s + 1) * DQ)
+                for t in range(PACK):
+                    nc.tensor.matmul_mx(
+                        out=dq[:, t, :],
+                        lhsT=eye_w[:, t * P:(t + 1) * P].bitcast(FP8X4),
+                        lhsT_scale=eye_s[:, t * P:(t + 1) * P],
+                        rhs=act_w[h][2][:, cols].bitcast(FP8X4),
+                        rhs_scale=act_s[h][2][:, cols],
+                        start=True,
+                        stop=True,
+                    )
+                nc.vector.tensor_tensor(
+                    r[:, s * PACK * DQ:(s + 1) * PACK * DQ].rearrange("p (j t) -> p j t", t=PACK),
+                    c_sb[u][:, :, s * DQ:(s + 1) * DQ].rearrange("p t j -> p j t"),
+                    dq[:].rearrange("p t j -> p j t"),
+                    SUB,
+                )
+            resid[u] = r
+
+        def tier_two(u):
+            quantise(resid[u], u // 2, 3, (u % 2) * CH)
+
+        def gather(q, h):
+            cols = slice(h * HALF // 16, (h + 1) * HALF // 16)
+            nc.vector.tensor_tensor(
+                gath[q // PACK][h][:, q % PACK, :], x_sb[q][:].indirect(offs_sb[:, cols]), wgt_sb[h][:], MULT
+            )
+
+        zs = {}
+
+        def x_interleave(a, h):
+            for s in range(HALF // CH):
+                zs[a, h, s] = interleave(gath[a][h][:, :, s * CH:(s + 1) * CH])
+
+        def x_quantise(a, h, s):
+            quantise(zs[a, h, s], h, a, s * CH)
+
+        acc = {}
+        order = (2, 3, 0, 1)
+
+        def product(m, h, o):
+            if o == order[0]:
+                acc[m, h] = psum.tile([P, HALF], F32, name="acc", tag="acc", bufs=5)
+            cols = slice(m * P, (m + 1) * P)
+            words = wt_w[:, o, cols] if o < 2 else wx_w[:, cols]
+            nc.tensor.matmul_mx(
+                out=acc[m, h][:],
+                lhsT=words.bitcast(FP8X4),
+                lhsT_scale=w_s[:, min(o, 2), cols],
+                rhs=act_w[h][o][:].bitcast(FP8X4),
+                rhs_scale=act_s[h][o][:],
+                start=(o == order[0]),
+                stop=(o == order[-1]),
+            )
+
+        ys = {}
+
+        def finish(m, h):
+            product(m, h, order[-1])
+            y = ring.tile([P, HALF], F32, name="y", tag="y", bufs=8)
+            nc.scalar.activation(out=y[:], in_=acc[m, h][:], func=IDENT, bias=bias[:, m:m + 1])
+            ys[m, h] = y
+
+        def scatter(m, h):
+            cols = slice(h * HALF // 16, (h + 1) * HALF // 16)
+            nc.vector.tensor_tensor(win[m % 3][:].indirect(offs2_sb[:, cols]), ys[m, h][:], wgo_sb[h][:], MULT)
+
+        def store(m):
+            nc.sync.dma_start(out=out[m * P:(m + 1) * P, :], in_=win[m % 3][:])
+
+        gather(0, 0)
+        gather(0, 1)
+        for u in range(4):
+            tier_one(u)
+            gather(u + 1, 0)
+            if u == 2:
+                x_interleave(0, 0)
+            residual(u)
+            if u < 3:
+                gather(u + 1, 1)
+            if u == 2:
+                x_interleave(0, 1)
+            if u == 3:
+                x_quantise(0, 0, 0)
+                x_quantise(0, 0, 1)
+            tier_two(u)
+        gather(5, 0)
+        x_quantise(0, 1, 0)
+        x_quantise(0, 1, 1)
+        gather(6, 0)
+        gather(7, 0)
+        x_interleave(1, 0)
+        for m in range(4):
+            for o in order[:-1]:
+                product(m, 0, o)
+        gather(4, 1)
+        gather(5, 1)
+        x_quantise(1, 0, 0)
+        x_quantise(1, 0, 1)
+        for m in range(4):
+            finish(m, 0)
+        gather(6, 1)
+        gather(7, 1)
+        x_interleave(1, 1)
+        scatter(0, 0)
+        x_quantise(1, 1, 0)
+        x_quantise(1, 1, 1)
+        for m in range(4):
+            for o in order[:-1]:
+                product(m, 1, o)
+            finish(m, 1)
+        scatter(1, 0)
+        scatter(0, 1)
+        store(0)
+        scatter(1, 1)
+        store(1)
+        scatter(2, 0)
+        scatter(2, 1)
+        store(2)
+        scatter(3, 0)
+        scatter(3, 1)
+        store(3)

@@ -16,6 +16,7 @@ FP8X4 = mybir.dt.float8_e4m3fn_x4
 MULT = mybir.AluOpType.mult
 SUB = mybir.AluOpType.subtract
 IDENT = mybir.ActivationFunctionType.Identity
+COPY = mybir.ActivationFunctionType.Copy
 
 P = 128
 PACK = 4
@@ -35,22 +36,25 @@ def tile_list_scatb_kernel(
 
         offs_sb = keep.tile([P, J // 16], U16, name="offs_sb")
         offs2_sb = keep.tile([P, J // 16], U16, name="offs2_sb")
-        x_sb = [keep.tile([P, T], F32, name="x%d" % q) for q in range(8)]
-        wgt_sb = [keep.tile([P, HALF], F32, name="wgt%d" % h) for h in range(2)]
+        x_sb = [keep.tile([P, T], F32, name="x%d" % q, tag="x%d" % q) for q in range(8)]
+        wgt_sb = [keep.tile([P, HALF], F32, name="wgt%d" % h, tag="wgt%d" % h) for h in range(2)]
         wgo_sb = [keep.tile([P, HALF], F32, name="wgo%d" % h) for h in range(2)]
         c_sb = [keep.tile([P, PACK, CH], F32, name="c%d" % u) for u in range(4)]
         wt_w = keep.tile([P, 2, N], U32, name="wt_w", align_bytes=64)
         wx_w = keep.tile([P, N], U32, name="wx_w", align_bytes=64)
         w_s = keep.tile([P, 3, N], U8, name="w_s", align_bytes=64)
         bias = keep.tile([P, N // P], F32, name="bias")
-        eye = keep.tile([P, P], BF16, name="eye")
+        eye = keep.tile([P, P], F32, name="eye")
         eye4 = keep.tile([P, PACK * (L + 1)], BF16, name="eye4", align_bytes=64)
         eye_w = keep.tile([P, L], U32, name="eye_w", align_bytes=64)
         eye_s = keep.tile([P, L], U8, name="eye_s", align_bytes=64)
-        act_w = [[keep.tile([P, HALF], U32, name="aw%d%d" % (h, o), align_bytes=64) for o in range(4)] for h in range(2)]
+        act_w = [[keep.tile([P, HALF], U32, name="aw%d%d" % (h, o), tag="aw%d%d" % (h, o), align_bytes=64) for o in range(4)] for h in range(2)]
         act_s = [[keep.tile([P, HALF], U8, name="as%d%d" % (h, o), align_bytes=64) for o in range(4)] for h in range(2)]
-        win = [keep.tile([P, T], F32, name="win%d" % w) for w in range(3)]
-        gath = [[keep.tile([P, PACK, HALF], F32, name="g%d%d" % (a, h)) for h in range(2)] for a in range(2)]
+        win = [keep.tile([P, T], F32, name="win%d" % w, tag=tag) for w, tag in enumerate(("win0", "win1", "x7", "wgt1"))]
+        gath = [
+            [keep.tile([P, PACK, HALF], F32, name="g%d%d" % (a, h), tag="wgt0" if a + h == 2 else "g%d%d" % (a, h)) for h in range(2)]
+            for a in range(2)
+        ]
 
         x_planes = xT.rearrange("(a p i) t -> a i p t", a=2, i=PACK)
         c_rows = c.rearrange("(p i) j -> p i j", i=PACK)
@@ -64,42 +68,32 @@ def tile_list_scatb_kernel(
         def load_half(tile, src, h):
             nc.sync.dma_start(out=tile[h][:], in_=src[:, h * HALF:(h + 1) * HALF])
 
-        def load_scales(q):
-            nc.sync.dma_start(
-                out=w_s[32 * q:32 * q + 4, 0:2, :].bitcast(I32),
-                in_=wt_scales[:, 4 * q:4 * q + 4, :].rearrange("a r n -> r a n").bitcast(I32),
-            )
-            nc.sync.dma_start(
-                out=w_s[32 * q:32 * q + 4, 2, :].bitcast(I32),
-                in_=wx_scales[0, 4 * q:4 * q + 4, :].bitcast(I32),
-            )
+        def load_scales(first, scales):
+            passes = scales.shape[0]
+            for q in range(4):
+                nc.sync.dma_start(
+                    out=w_s[32 * q:32 * q + 4, first:first + passes, :].bitcast(I32),
+                    in_=scales[:, 4 * q:4 * q + 4, :].rearrange("a r n -> r a n").bitcast(I32),
+                )
 
         nc.vector.memset(w_s[:].rearrange("p a n -> p (a n)").bitcast(I32), 0)
         nc.sync.dma_start(offs_sb[:], offs)
         load_half(wgt_sb, wgt, 0)
         load_x(0)
         load_half(wgt_sb, wgt, 1)
-        load_c(0)
-        load_x(1)
-        load_c(1)
-        load_x(2)
-        load_c(2)
-        load_x(3)
-        load_c(3)
-        load_x(4)
-        load_x(5)
-        load_scales(0)
-        load_scales(1)
-        load_x(6)
-        load_scales(2)
-        load_scales(3)
-        load_x(7)
-        nc.sync.dma_start(out=wx_w[:].bitcast(I32), in_=wx_words[0].rearrange("p n i -> p (n i)").bitcast(I32))
+        for u in range(4):
+            load_c(u)
+            load_x(u + 1)
+        for q in range(5, 8):
+            load_x(q)
         nc.sync.dma_start(out=wt_w[:].bitcast(I32), in_=wt_words.rearrange("a p n i -> p a (n i)").bitcast(I32))
-        nc.sync.dma_start(offs2_sb[:], offs2)
-        load_half(wgo_sb, wgo, 0)
+        load_scales(2, wx_scales)
+        nc.sync.dma_start(out=wx_w[:].bitcast(I32), in_=wx_words[0].rearrange("p n i -> p (n i)").bitcast(I32))
+        load_scales(0, wt_scales)
         with nc.allow_non_contiguous_dma(reason="one bias value to a partition and output tile"):
             nc.sync.dma_start(out=bias[:], in_=b.rearrange("(m p) -> p m", p=P))
+        nc.sync.dma_start(offs2_sb[:], offs2)
+        load_half(wgo_sb, wgo, 0)
         load_half(wgo_sb, wgo, 1)
 
         make_identity(nc, eye[:])
@@ -109,37 +103,74 @@ def tile_list_scatb_kernel(
             out=eye4[:].rearrange("p (t x) -> p t x", t=PACK)[:, :, 0:L:PACK],
             in_=eye[:].unsqueeze(1).to_broadcast([P, PACK, P]),
         )
-        nc.vector.memset(win[0][:], 0.0)
-        nc.vector.memset(win[1][:], 0.0)
-        nc.vector.memset(win[2][:], 0.0)
+        for w in range(2):
+            nc.vector.memset(win[w][:], 0.0)
         nc.vector.quantize_mx(out=eye_w[:].bitcast(FP8X4), scales=eye_s[:], in_=eye4[:, 0:PACK * L])
 
         def by_fours_src(ap):
-            return ap.rearrange("p t (g e) -> p g t e", e=4)
+            return ap.rearrange("p t (g e) -> p g t e", e=2)
 
         def by_fours_dst(ap):
-            return ap.rearrange("p (g e t) -> p g t e", e=4, t=PACK)
+            return ap.rearrange("p (g e t) -> p g t e", e=2, t=PACK)
 
-        def interleave(src):
-            z = ring.tile([P, PACK * CH], BF16, name="z", tag="z", bufs=6, align_bytes=64)
+        def interleave(src, z=None):
+            if z is None:
+                z = ring.tile([P, PACK * CH], BF16, name="z", tag="z", bufs=6, align_bytes=64)
             nc.scalar.copy(out=by_fours_dst(z[:]), in_=by_fours_src(src))
             return z
 
         def quantise(z, h, o, j0):
-            nc.vector.quantize_mx(
-                out=act_w[h][o][:, j0:j0 + CH].bitcast(FP8X4), scales=act_s[h][o][:, j0:j0 + CH], in_=z[:]
-            )
+            cols = slice(j0, j0 + z.shape[1] // PACK)
+            nc.vector.quantize_mx(out=act_w[h][o][:, cols].bitcast(FP8X4), scales=act_s[h][o][:, cols], in_=z[:])
 
         resid = {}
 
         def tier_one(u):
             quantise(interleave(c_sb[u][:]), u // 2, 2, (u % 2) * CH)
 
+        turned = {}
+
+        def turn_c(u):
+            for s in range(CH // DQ):
+                bank = psum.tile([P, PACK, P], F32, name="turn", tag="turn", bufs=1)
+                for t in range(PACK):
+                    nc.tensor.transpose(bank[:, t, :], c_sb[u][:, t, s * DQ:(s + 1) * DQ], eye[:])
+                ct = ring.tile([P, PACK, P], F32, name="ct", tag="ct", bufs=4)
+                nc.scalar.copy(out=ct[:], in_=bank[:])
+                turned[u, s] = ct
+
         def residual(u):
             h, j0 = u // 2, (u % 2) * CH
             r = ring.tile([P, PACK * CH], BF16, name="r", tag="r", bufs=2, align_bytes=64)
             for s in range(CH // DQ):
-                dq = psum.tile([P, PACK, DQ], F32, name="dq", tag="dq", bufs=3)
+                cols = slice(j0 + s * DQ, j0 + (s + 1) * DQ)
+                dq = psum.tile([P, L], F32, name="dq", tag="dq", bufs=2)
+                nc.tensor.matmul_mx(
+                    out=dq[:],
+                    lhsT=act_w[h][2][:, cols].bitcast(FP8X4),
+                    lhsT_scale=act_s[h][2][:, cols],
+                    rhs=eye_w[:].bitcast(FP8X4),
+                    rhs_scale=eye_s[:],
+                    start=True,
+                    stop=True,
+                )
+                nq = ring.tile([P, L], F32, name="nq", tag="nq", bufs=2)
+                nc.scalar.activation(out=nq[:], in_=dq[:], func=COPY, scale=-1.0)
+                diff = psum.tile([P, PACK, DQ], F32, name="diff", tag="diff", bufs=2)
+                for t in range(PACK):
+                    nc.tensor.matmul(diff[:, t, :], lhsT=turned[u, s][:, t, :], rhs=eye[:], start=True, stop=False, is_transpose=True)
+                    nc.tensor.matmul(diff[:, t, :], lhsT=nq[:, t * P:(t + 1) * P], rhs=eye[:], start=False, stop=True, is_transpose=True)
+                nc.scalar.copy(
+                    out=by_fours_dst(r[:, s * PACK * DQ:(s + 1) * PACK * DQ]),
+                    in_=by_fours_src(diff[:]),
+                )
+            resid[u] = r
+
+        def residual_on_vector(u):
+            h, j0 = u // 2, (u % 2) * CH
+            r = ring.tile([P, PACK * CH], BF16, name="r", tag="r", bufs=2, align_bytes=64)
+            for s in range(CH // DQ):
+                dq = psum.tile([P, PACK, DQ], F32, name="dq", tag="dq", bufs=2)
                 cols = slice(j0 + s * DQ, j0 + (s + 1) * DQ)
                 for t in range(PACK):
                     nc.tensor.matmul_mx(
@@ -152,9 +183,9 @@ def tile_list_scatb_kernel(
                         stop=True,
                     )
                 nc.vector.tensor_tensor(
-                    r[:, s * PACK * DQ:(s + 1) * PACK * DQ].rearrange("p (j t) -> p j t", t=PACK),
-                    c_sb[u][:, :, s * DQ:(s + 1) * DQ].rearrange("p t j -> p j t"),
-                    dq[:].rearrange("p t j -> p j t"),
+                    by_fours_dst(r[:, s * PACK * DQ:(s + 1) * PACK * DQ]),
+                    by_fours_src(c_sb[u][:, :, s * DQ:(s + 1) * DQ]),
+                    by_fours_src(dq[:]),
                     SUB,
                 )
             resid[u] = r
@@ -182,7 +213,7 @@ def tile_list_scatb_kernel(
 
         def product(m, h, o):
             if o == order[0]:
-                acc[m, h] = psum.tile([P, HALF], F32, name="acc", tag="acc", bufs=5)
+                acc[m, h] = psum.tile([P, HALF], F32, name="acc", tag="acc", bufs=3)
             cols = slice(m * P, (m + 1) * P)
             words = wt_w[:, o, cols] if o < 2 else wx_w[:, cols]
             nc.tensor.matmul_mx(
@@ -199,66 +230,85 @@ def tile_list_scatb_kernel(
 
         def finish(m, h):
             product(m, h, order[-1])
+            empty(m, h)
+
+        def empty(m, h):
             y = ring.tile([P, HALF], F32, name="y", tag="y", bufs=8)
             nc.scalar.activation(out=y[:], in_=acc[m, h][:], func=IDENT, bias=bias[:, m:m + 1])
             ys[m, h] = y
 
         def scatter(m, h):
             cols = slice(h * HALF // 16, (h + 1) * HALF // 16)
-            nc.vector.tensor_tensor(win[m % 3][:].indirect(offs2_sb[:, cols]), ys[m, h][:], wgo_sb[h][:], MULT)
+            nc.vector.tensor_tensor(win[m][:].indirect(offs2_sb[:, cols]), ys[m, h][:], wgo_sb[h][:], MULT)
 
         def store(m):
-            nc.sync.dma_start(out=out[m * P:(m + 1) * P, :], in_=win[m % 3][:])
+            nc.sync.dma_start(out=out[m * P:(m + 1) * P, :], in_=win[m][:])
 
         gather(0, 0)
         gather(0, 1)
-        for u in range(4):
-            tier_one(u)
-            gather(u + 1, 0)
-            if u == 2:
-                x_interleave(0, 0)
-            residual(u)
-            if u < 3:
-                gather(u + 1, 1)
-            if u == 2:
-                x_interleave(0, 1)
-            if u == 3:
-                x_quantise(0, 0, 0)
-                x_quantise(0, 0, 1)
-            tier_two(u)
+        tier_one(0)
+        gather(1, 0)
+        residual_on_vector(0)
+        gather(1, 1)
+        tier_two(0)
+        tier_one(1)
+        turn_c(1)
+        gather(2, 0)
+        residual(1)
+        gather(2, 1)
+        tier_one(2)
+        turn_c(2)
+        tier_two(1)
+        gather(3, 0)
+        residual(2)
+        gather(3, 1)
+        tier_one(3)
+        x_interleave(0, 0)
+        gather(4, 0)
+        tier_two(2)
         gather(5, 0)
-        x_quantise(0, 1, 0)
-        x_quantise(0, 1, 1)
+        x_quantise(0, 0, 0)
+        x_quantise(0, 0, 1)
+        turn_c(3)
         gather(6, 0)
         gather(7, 0)
         x_interleave(1, 0)
-        for m in range(4):
+        for m in range(3):
             for o in order[:-1]:
                 product(m, 0, o)
         gather(4, 1)
         gather(5, 1)
         x_quantise(1, 0, 0)
-        x_quantise(1, 0, 1)
-        for m in range(4):
-            finish(m, 0)
         gather(6, 1)
+        x_quantise(1, 0, 1)
         gather(7, 1)
-        x_interleave(1, 1)
+        for w in range(2, 4):
+            nc.gpsimd.memset(win[w][:], 0.0)
+        finish(0, 0)
+        finish(1, 0)
+        product(2, 0, order[-1])
+        for o in order:
+            product(3, 0, o)
+        residual(3)
+        x_interleave(0, 1)
+        z_last = keep.tile([P, PACK * HALF], BF16, name="z_last", tag="aw02", align_bytes=64)
+        interleave(gath[1][1][:], z_last)
+        empty(2, 0)
+        empty(3, 0)
         scatter(0, 0)
-        x_quantise(1, 1, 0)
-        x_quantise(1, 1, 1)
+        x_quantise(0, 1, 0)
+        x_quantise(0, 1, 1)
+        tier_two(3)
+        scatter(1, 0)
+        quantise(z_last, 1, 1, 0)
         for m in range(4):
             for o in order[:-1]:
                 product(m, 1, o)
             finish(m, 1)
-        scatter(1, 0)
-        scatter(0, 1)
-        store(0)
-        scatter(1, 1)
-        store(1)
         scatter(2, 0)
-        scatter(2, 1)
-        store(2)
         scatter(3, 0)
+        for m in range(3):
+            scatter(m, 1)
+            store(m)
         scatter(3, 1)
         store(3)

@@ -23,6 +23,28 @@ PACK = 4
 HALF = J // 2
 CH = 256
 DQ = 128
+MERGE = (1, 1)
+RTAG = ('x3', 'x5')
+HEAD = 1
+ZV = ()
+W00 = 1
+W01 = 0
+EARLY = 0
+MSP = 1
+WT = ('win0', 'win1', 'y0', 'y1')
+HOLD4 = 1
+LATE_POS = 2
+LATE_FROM = 7
+VEC = (1,)
+RB = 2
+NQB = 2
+CTB = 4
+HOLD01 = 0
+TURN = ('dq', 3)
+DQB = 3
+DIFFB = 2
+ACCB = 3
+LOADS = [('c', 0), ('w', 0), ('x', 0), ('w', 1), ('c', 1), ('x', 1), ('c', 2), ('x', 2), ('c', 3), ('x', 3), ('x', 4), ('x', 5), ('x', 6), ('x', 7)]
 
 
 def tile_list_scatb_kernel(
@@ -36,10 +58,12 @@ def tile_list_scatb_kernel(
 
         offs_sb = keep.tile([P, J // 16], U16, name="offs_sb")
         offs2_sb = keep.tile([P, J // 16], U16, name="offs2_sb")
-        x_sb = [keep.tile([P, T], F32, name="x%d" % q, tag="x%d" % q) for q in range(8)]
+        x_sb = [keep.tile([P, T], F32, name="x%d" % q, tag="x%d" % q, align_bytes=64) for q in range(8)]
         wgt_sb = [keep.tile([P, HALF], F32, name="wgt%d" % h, tag="wgt%d" % h) for h in range(2)]
+        wgt_late = keep.tile([P, HALF], F32, name="wgt_late", tag="wgt_late")
         wgo_sb = [keep.tile([P, HALF], F32, name="wgo%d" % h) for h in range(2)]
-        c_sb = [keep.tile([P, PACK, CH], F32, name="c%d" % u) for u in range(4)]
+        c_sb = [keep.tile([P, PACK, CH], F32, name="c%d" % u, tag="c%d" % u) for u in range(4)]
+        r_half = [keep.tile([P, PACK * HALF], BF16, name="r%d" % h, align_bytes=64) for h in range(2)]
         wt_w = keep.tile([P, 2, N], U32, name="wt_w", align_bytes=64)
         wx_w = keep.tile([P, N], U32, name="wx_w", align_bytes=64)
         w_s = keep.tile([P, 3, N], U8, name="w_s", align_bytes=64)
@@ -48,12 +72,19 @@ def tile_list_scatb_kernel(
         eye4 = keep.tile([P, PACK * (L + 1)], BF16, name="eye4", align_bytes=64)
         eye_w = keep.tile([P, L], U32, name="eye_w", align_bytes=64)
         eye_s = keep.tile([P, L], U8, name="eye_s", align_bytes=64)
-        act_w = [[keep.tile([P, HALF], U32, name="aw%d%d" % (h, o), tag="aw%d%d" % (h, o), align_bytes=64) for o in range(4)] for h in range(2)]
-        act_s = [[keep.tile([P, HALF], U8, name="as%d%d" % (h, o), align_bytes=64) for o in range(4)] for h in range(2)]
-        win = [keep.tile([P, T], F32, name="win%d" % w, tag=tag) for w, tag in enumerate(("win0", "win1", "x7", "wgt1"))]
+        act_w = [[keep.tile([P, HALF], U32, name="aw%d%d" % (h, o), tag=RTAG[h] if o == 3 and RTAG[h] else "aw%d%d" % (h, o), align_bytes=64) for o in range(4)] for h in range(2)]
+        act_s = [[keep.tile([P, HALF], U8, name="as%d%d" % (h, o), tag="as%d%d" % (h, o), align_bytes=64) for o in range(4)] for h in range(2)]
+        y_first = [keep.tile([P, HALF], F32, name="y%d" % m, tag="y%d" % m) for m in range(2)]
+        win = [keep.tile([P, T], F32, name="win%d" % w, tag=tag) for w, tag in enumerate(WT)]
         gath = [
-            [keep.tile([P, PACK, HALF], F32, name="g%d%d" % (a, h), tag="wgt0" if a + h == 2 else "g%d%d" % (a, h)) for h in range(2)]
-            for a in range(2)
+            [
+                keep.tile([P, PACK, HALF], F32, name="g00", tag="c0" if HEAD & 1 else "g00"),
+                keep.tile([P, PACK, HALF], F32, name="g01", tag="g01"),
+            ],
+            [
+                keep.tile([P, PACK, HALF], F32, name="g10"),
+                keep.tile([P, PACK, HALF], F32, name="g11", tag="wgt0" if HOLD4 else "g11"),
+            ],
         ]
 
         x_planes = xT.rearrange("(a p i) t -> a i p t", a=2, i=PACK)
@@ -78,14 +109,15 @@ def tile_list_scatb_kernel(
 
         nc.vector.memset(w_s[:].rearrange("p a n -> p (a n)").bitcast(I32), 0)
         nc.sync.dma_start(offs_sb[:], offs)
-        load_half(wgt_sb, wgt, 0)
-        load_x(0)
-        load_half(wgt_sb, wgt, 1)
-        for u in range(4):
-            load_c(u)
-            load_x(u + 1)
-        for q in range(5, 8):
-            load_x(q)
+        for kind, q in LOADS:
+            if kind == "x":
+                load_x(q)
+            elif kind == "c":
+                load_c(q)
+            else:
+                load_half(wgt_sb, wgt, q)
+        if LATE_POS == 0:
+            nc.sync.dma_start(out=wgt_late[:], in_=wgt[:, HALF:J])
         nc.sync.dma_start(out=wt_w[:].bitcast(I32), in_=wt_words.rearrange("a p n i -> p a (n i)").bitcast(I32))
         load_scales(2, wx_scales)
         nc.sync.dma_start(out=wx_w[:].bitcast(I32), in_=wx_words[0].rearrange("p n i -> p (n i)").bitcast(I32))
@@ -94,7 +126,11 @@ def tile_list_scatb_kernel(
             nc.sync.dma_start(out=bias[:], in_=b.rearrange("(m p) -> p m", p=P))
         nc.sync.dma_start(offs2_sb[:], offs2)
         load_half(wgo_sb, wgo, 0)
+        if LATE_POS == 1:
+            nc.sync.dma_start(out=wgt_late[:], in_=wgt[:, HALF:J])
         load_half(wgo_sb, wgo, 1)
+        if LATE_POS == 2:
+            nc.sync.dma_start(out=wgt_late[:], in_=wgt[:, HALF:J])
 
         make_identity(nc, eye[:])
 
@@ -113,38 +149,37 @@ def tile_list_scatb_kernel(
         def by_fours_dst(ap):
             return ap.rearrange("p (g e t) -> p g t e", e=2, t=PACK)
 
-        def interleave(src, z=None):
+        def interleave(src, z=None, on_vector=False):
             if z is None:
                 z = ring.tile([P, PACK * CH], BF16, name="z", tag="z", bufs=6, align_bytes=64)
-            nc.scalar.copy(out=by_fours_dst(z[:]), in_=by_fours_src(src))
+            copy = nc.vector.tensor_copy if on_vector else nc.scalar.copy
+            copy(out=by_fours_dst(z[:]), in_=by_fours_src(src))
             return z
 
         def quantise(z, h, o, j0):
             cols = slice(j0, j0 + z.shape[1] // PACK)
             nc.vector.quantize_mx(out=act_w[h][o][:, cols].bitcast(FP8X4), scales=act_s[h][o][:, cols], in_=z[:])
 
-        resid = {}
-
         def tier_one(u):
-            quantise(interleave(c_sb[u][:]), u // 2, 2, (u % 2) * CH)
+            quantise(interleave(c_sb[u][:], on_vector=u in ZV), u // 2, 2, (u % 2) * CH)
 
         turned = {}
 
         def turn_c(u):
             for s in range(CH // DQ):
-                bank = psum.tile([P, PACK, P], F32, name="turn", tag="turn", bufs=1)
+                bank = psum.tile([P, PACK, P], F32, name="turn", tag=TURN[0], bufs=TURN[1])
                 for t in range(PACK):
                     nc.tensor.transpose(bank[:, t, :], c_sb[u][:, t, s * DQ:(s + 1) * DQ], eye[:])
-                ct = ring.tile([P, PACK, P], F32, name="ct", tag="ct", bufs=4)
+                ct = ring.tile([P, PACK, P], F32, name="ct", tag="ct", bufs=CTB)
                 nc.scalar.copy(out=ct[:], in_=bank[:])
                 turned[u, s] = ct
 
         def residual(u):
             h, j0 = u // 2, (u % 2) * CH
-            r = ring.tile([P, PACK * CH], BF16, name="r", tag="r", bufs=2, align_bytes=64)
+            r = r_half[h][:, PACK * j0:PACK * (j0 + CH)]
             for s in range(CH // DQ):
                 cols = slice(j0 + s * DQ, j0 + (s + 1) * DQ)
-                dq = psum.tile([P, L], F32, name="dq", tag="dq", bufs=2)
+                dq = psum.tile([P, L], F32, name="dq", tag="dq", bufs=DQB)
                 nc.tensor.matmul_mx(
                     out=dq[:],
                     lhsT=act_w[h][2][:, cols].bitcast(FP8X4),
@@ -154,23 +189,28 @@ def tile_list_scatb_kernel(
                     start=True,
                     stop=True,
                 )
-                nq = ring.tile([P, L], F32, name="nq", tag="nq", bufs=2)
+                nq = ring.tile([P, L], F32, name="nq", tag="nq", bufs=NQB)
                 nc.scalar.activation(out=nq[:], in_=dq[:], func=COPY, scale=-1.0)
-                diff = psum.tile([P, PACK, DQ], F32, name="diff", tag="diff", bufs=2)
-                for t in range(PACK):
-                    nc.tensor.matmul(diff[:, t, :], lhsT=turned[u, s][:, t, :], rhs=eye[:], start=True, stop=False, is_transpose=True)
-                    nc.tensor.matmul(diff[:, t, :], lhsT=nq[:, t * P:(t + 1) * P], rhs=eye[:], start=False, stop=True, is_transpose=True)
+                diff = psum.tile([P, PACK, DQ], F32, name="diff", tag="diff", bufs=DIFFB)
+                if EARLY:
+                    for t in range(PACK):
+                        nc.tensor.matmul(diff[:, t, :], lhsT=turned[u, s][:, t, :], rhs=eye[:], start=(t == 0), stop=False, is_transpose=True)
+                    for t in range(PACK):
+                        nc.tensor.matmul(diff[:, t, :], lhsT=nq[:, t * P:(t + 1) * P], rhs=eye[:], start=False, stop=(t == PACK - 1), is_transpose=True)
+                else:
+                    for t in range(PACK):
+                        nc.tensor.matmul(diff[:, t, :], lhsT=turned[u, s][:, t, :], rhs=eye[:], start=True, stop=False, is_transpose=True)
+                        nc.tensor.matmul(diff[:, t, :], lhsT=nq[:, t * P:(t + 1) * P], rhs=eye[:], start=False, stop=True, is_transpose=True)
                 nc.scalar.copy(
                     out=by_fours_dst(r[:, s * PACK * DQ:(s + 1) * PACK * DQ]),
                     in_=by_fours_src(diff[:]),
                 )
-            resid[u] = r
 
         def residual_on_vector(u):
             h, j0 = u // 2, (u % 2) * CH
-            r = ring.tile([P, PACK * CH], BF16, name="r", tag="r", bufs=2, align_bytes=64)
+            r = r_half[h][:, PACK * j0:PACK * (j0 + CH)]
             for s in range(CH // DQ):
-                dq = psum.tile([P, PACK, DQ], F32, name="dq", tag="dq", bufs=2)
+                dq = psum.tile([P, PACK, DQ], F32, name="dq", tag="dq", bufs=DQB)
                 cols = slice(j0 + s * DQ, j0 + (s + 1) * DQ)
                 for t in range(PACK):
                     nc.tensor.matmul_mx(
@@ -188,15 +228,18 @@ def tile_list_scatb_kernel(
                     by_fours_src(dq[:]),
                     SUB,
                 )
-            resid[u] = r
 
         def tier_two(u):
-            quantise(resid[u], u // 2, 3, (u % 2) * CH)
+            h, j0 = u // 2, (u % 2) * CH
+            if not MERGE[h]:
+                quantise(r_half[h][:, PACK * j0:PACK * (j0 + CH)], h, 3, j0)
+            elif j0:
+                quantise(r_half[h], h, 3, 0)
 
         def gather(q, h):
             cols = slice(h * HALF // 16, (h + 1) * HALF // 16)
             nc.vector.tensor_tensor(
-                gath[q // PACK][h][:, q % PACK, :], x_sb[q][:].indirect(offs_sb[:, cols]), wgt_sb[h][:], MULT
+                gath[q // PACK][h][:, q % PACK, :], x_sb[q][:].indirect(offs_sb[:, cols]), (wgt_late if h == 1 and q >= LATE_FROM else wgt_sb[h])[:], MULT
             )
 
         zs = {}
@@ -213,7 +256,7 @@ def tile_list_scatb_kernel(
 
         def product(m, h, o):
             if o == order[0]:
-                acc[m, h] = psum.tile([P, HALF], F32, name="acc", tag="acc", bufs=3)
+                acc[m, h] = psum.tile([P, HALF], F32, name="acc", tag="acc", bufs=ACCB)
             cols = slice(m * P, (m + 1) * P)
             words = wt_w[:, o, cols] if o < 2 else wx_w[:, cols]
             nc.tensor.matmul_mx(
@@ -233,7 +276,7 @@ def tile_list_scatb_kernel(
             empty(m, h)
 
         def empty(m, h):
-            y = ring.tile([P, HALF], F32, name="y", tag="y", bufs=8)
+            y = y_first[m] if h == 0 and m < 2 else ring.tile([P, HALF], F32, name="y", tag="y", bufs=6)
             nc.scalar.activation(out=y[:], in_=acc[m, h][:], func=IDENT, bias=bias[:, m:m + 1])
             ys[m, h] = y
 
@@ -244,71 +287,68 @@ def tile_list_scatb_kernel(
         def store(m):
             nc.sync.dma_start(out=out[m * P:(m + 1) * P, :], in_=win[m][:])
 
-        gather(0, 0)
-        gather(0, 1)
-        tier_one(0)
-        gather(1, 0)
-        residual_on_vector(0)
-        gather(1, 1)
-        tier_two(0)
-        tier_one(1)
-        turn_c(1)
-        gather(2, 0)
-        residual(1)
-        gather(2, 1)
-        tier_one(2)
-        turn_c(2)
-        tier_two(1)
-        gather(3, 0)
-        residual(2)
-        gather(3, 1)
-        tier_one(3)
-        x_interleave(0, 0)
-        gather(4, 0)
-        tier_two(2)
-        gather(5, 0)
-        x_quantise(0, 0, 0)
-        x_quantise(0, 0, 1)
-        turn_c(3)
-        gather(6, 0)
-        gather(7, 0)
+        def chunk(u):
+            tier_one(u)
+            if u in VEC:
+                residual_on_vector(u)
+            else:
+                turn_c(u)
+                residual(u)
+            tier_two(u)
+
+        chunk(0)
+        for q in range(4):
+            gather(q, 0)
+            if q == 3 and W00:
+                z_wide = keep.tile([P, PACK * HALF], BF16, name="z_wide", align_bytes=64)
+                interleave(gath[0][0][:], z_wide)
+                quantise(z_wide, 0, 0, 0)
+            elif q == 3:
+                x_interleave(0, 0)
+                x_quantise(0, 0, 0)
+                x_quantise(0, 0, 1)
+            gather(q, 1)
+            if q > 0:
+                chunk(q)
+        for q in range(4, 8):
+            gather(q, 0)
         x_interleave(1, 0)
-        for m in range(3):
+        for m in range(ACCB):
             for o in order[:-1]:
                 product(m, 0, o)
-        gather(4, 1)
-        gather(5, 1)
         x_quantise(1, 0, 0)
-        gather(6, 1)
         x_quantise(1, 0, 1)
-        gather(7, 1)
-        for w in range(2, 4):
-            nc.gpsimd.memset(win[w][:], 0.0)
-        finish(0, 0)
-        finish(1, 0)
-        product(2, 0, order[-1])
-        for o in order:
-            product(3, 0, o)
-        residual(3)
-        x_interleave(0, 1)
+        for q in range(4, 8):
+            gather(q, 1)
+        for m in range(4):
+            if m >= ACCB:
+                for o in order[:-1]:
+                    product(m, 0, o)
+            finish(m, 0)
+        if HOLD01:
+            z_first = keep.tile([P, PACK * HALF], BF16, name="z_first", tag="as02", align_bytes=64)
+            interleave(gath[0][1][:], z_first)
+            quantise(z_first, 1, 0, 0)
+        elif W01:
+            z_first = keep.tile([P, PACK * HALF], BF16, name="z_first", align_bytes=64)
+            interleave(gath[0][1][:], z_first)
+            quantise(z_first, 1, 0, 0)
+        else:
+            x_interleave(0, 1)
+            x_quantise(0, 1, 0)
+            x_quantise(0, 1, 1)
         z_last = keep.tile([P, PACK * HALF], BF16, name="z_last", tag="aw02", align_bytes=64)
         interleave(gath[1][1][:], z_last)
-        empty(2, 0)
-        empty(3, 0)
-        scatter(0, 0)
-        x_quantise(0, 1, 0)
-        x_quantise(0, 1, 1)
-        tier_two(3)
-        scatter(1, 0)
         quantise(z_last, 1, 1, 0)
         for m in range(4):
             for o in order[:-1]:
                 product(m, 1, o)
             finish(m, 1)
-        scatter(2, 0)
-        scatter(3, 0)
-        for m in range(3):
+        for m in range(4):
+            if m >= 2:
+                for s in range(MSP):
+                    nc.gpsimd.memset(win[m][:, s * T // MSP:(s + 1) * T // MSP], 0.0)
+            scatter(m, 0)
+        for m in range(4):
             scatter(m, 1)
             store(m)
-        scatter(3, 1)
-        store(3)

@@ -14,37 +14,16 @@ U16 = mybir.dt.uint16
 U8 = mybir.dt.uint8
 FP8X4 = mybir.dt.float8_e4m3fn_x4
 MULT = mybir.AluOpType.mult
-SUB = mybir.AluOpType.subtract
 IDENT = mybir.ActivationFunctionType.Identity
 COPY = mybir.ActivationFunctionType.Copy
 
 P = 128
 PACK = 4
 HALF = J // 2
-CH = 256
-DQ = 128
-MERGE = (1, 1)
-RTAG = ('x3', 'x5')
-HEAD = 1
-ZV = ()
-W00 = 1
-W01 = 0
-EARLY = 0
-MSP = 1
-WT = ('win0', 'win1', 'y0', 'y1')
-HOLD4 = 1
-LATE_POS = 2
-LATE_FROM = 7
-VEC = (1,)
-RB = 2
-NQB = 2
-CTB = 4
-HOLD01 = 0
-TURN = ('dq', 3)
-DQB = 3
-DIFFB = 2
-ACCB = 3
-LOADS = [('c', 0), ('w', 0), ('x', 0), ('w', 1), ('c', 1), ('x', 1), ('c', 2), ('x', 2), ('c', 3), ('x', 3), ('x', 4), ('x', 5), ('x', 6), ('x', 7)]
+QUARTER = J // 4
+BANK = 512
+ROW_TILES = N // P
+A, B, C = slice(0, QUARTER), slice(QUARTER, HALF), slice(HALF, J)
 
 
 def tile_list_scatb_kernel(
@@ -52,40 +31,36 @@ def tile_list_scatb_kernel(
 ):
     nc = tc.nc
     with ExitStack() as ctx:
+        lists = ctx.enter_context(tc.tile_pool(name="lists", bufs=1))
         keep = ctx.enter_context(tc.tile_pool(name="keep", bufs=1))
-        ring = ctx.enter_context(tc.tile_pool(name="ring", bufs=3))
         psum = ctx.enter_context(tc.psum_pool(name="psum", bufs=1))
 
-        offs_sb = keep.tile([P, J // 16], U16, name="offs_sb")
-        offs2_sb = keep.tile([P, J // 16], U16, name="offs2_sb")
-        x_sb = [keep.tile([P, T], F32, name="x%d" % q, tag="x%d" % q, align_bytes=64) for q in range(8)]
-        wgt_sb = [keep.tile([P, HALF], F32, name="wgt%d" % h, tag="wgt%d" % h) for h in range(2)]
-        wgt_late = keep.tile([P, HALF], F32, name="wgt_late", tag="wgt_late")
-        wgo_sb = [keep.tile([P, HALF], F32, name="wgo%d" % h) for h in range(2)]
-        c_sb = [keep.tile([P, PACK, CH], F32, name="c%d" % u, tag="c%d" % u) for u in range(4)]
-        r_half = [keep.tile([P, PACK * HALF], BF16, name="r%d" % h, align_bytes=64) for h in range(2)]
-        wt_w = keep.tile([P, 2, N], U32, name="wt_w", align_bytes=64)
-        wx_w = keep.tile([P, N], U32, name="wx_w", align_bytes=64)
-        w_s = keep.tile([P, 3, N], U8, name="w_s", align_bytes=64)
-        bias = keep.tile([P, N // P], F32, name="bias")
-        eye = keep.tile([P, P], F32, name="eye")
-        eye4 = keep.tile([P, PACK * (L + 1)], BF16, name="eye4", align_bytes=64)
-        eye_w = keep.tile([P, L], U32, name="eye_w", align_bytes=64)
-        eye_s = keep.tile([P, L], U8, name="eye_s", align_bytes=64)
-        act_w = [[keep.tile([P, HALF], U32, name="aw%d%d" % (h, o), tag=RTAG[h] if o == 3 and RTAG[h] else "aw%d%d" % (h, o), align_bytes=64) for o in range(4)] for h in range(2)]
-        act_s = [[keep.tile([P, HALF], U8, name="as%d%d" % (h, o), tag="as%d%d" % (h, o), align_bytes=64) for o in range(4)] for h in range(2)]
-        y_first = [keep.tile([P, HALF], F32, name="y%d" % m, tag="y%d" % m) for m in range(2)]
-        win = [keep.tile([P, T], F32, name="win%d" % w, tag=tag) for w, tag in enumerate(WT)]
-        gath = [
-            [
-                keep.tile([P, PACK, HALF], F32, name="g00", tag="c0" if HEAD & 1 else "g00"),
-                keep.tile([P, PACK, HALF], F32, name="g01", tag="g01"),
-            ],
-            [
-                keep.tile([P, PACK, HALF], F32, name="g10"),
-                keep.tile([P, PACK, HALF], F32, name="g11", tag="wgt0" if HOLD4 else "g11"),
-            ],
-        ]
+        def sb(name, shape, dtype, tag=None):
+            return keep.tile(shape, dtype, name=name, tag=tag or name, align_bytes=64)
+
+        def bank(name, n):
+            return psum.tile([P, BANK], F32, name=name, tag="bank%d" % n)
+
+        def width(cols):
+            return cols.stop - cols.start
+
+        def list_cols(cols):
+            return slice(cols.start // 16, cols.stop // 16)
+
+        offs_sb = lists.tile([P, J // 16], U16, name="offs_sb")
+        offs2_sb = lists.tile([P, J // 16], U16, name="offs2_sb")
+        x_sb = [sb("x%d" % q, [P, T], F32) for q in range(2 * PACK)]
+        c_sb = [sb("c%d" % h, [P, PACK, HALF], F32) for h in range(2)]
+        wgt_sb = sb("wgt", [P, J], F32)
+        wgo_sb = sb("wgo", [P, J], F32)
+        wt_w = sb("wt_w", [P, 2, N], U32)
+        wx_w = sb("wx_w", [P, N], U32)
+        bias = sb("bias", [P, ROW_TILES], F32)
+        eye = sb("eye", [P, P], F32)
+        eye4 = sb("eye4", [P, PACK * (L + 1)], BF16)
+        eye_w = sb("eye_w", [P, L], U32)
+        eye_s = sb("eye_s", [P, L], U8)
+        win = [sb("win%d" % m, [P, T], F32) for m in range(ROW_TILES)]
 
         x_planes = xT.rearrange("(a p i) t -> a i p t", a=2, i=PACK)
         c_rows = c.rearrange("(p i) j -> p i j", i=PACK)
@@ -93,262 +68,202 @@ def tile_list_scatb_kernel(
         def load_x(q):
             nc.sync.dma_start(out=x_sb[q][:], in_=x_planes[q // PACK, q % PACK])
 
-        def load_c(u):
-            nc.sync.dma_start(out=c_sb[u][:], in_=c_rows[:, :, u * CH:(u + 1) * CH])
+        def load_c(h):
+            nc.sync.dma_start(out=c_sb[h][:], in_=c_rows[:, :, h * HALF:(h + 1) * HALF])
 
         def load_half(tile, src, h):
-            nc.sync.dma_start(out=tile[h][:], in_=src[:, h * HALF:(h + 1) * HALF])
+            nc.sync.dma_start(out=tile[:, h * HALF:(h + 1) * HALF], in_=src[:, h * HALF:(h + 1) * HALF])
 
-        def load_scales(first, scales):
-            passes = scales.shape[0]
-            for q in range(4):
-                nc.sync.dma_start(
-                    out=w_s[32 * q:32 * q + 4, first:first + passes, :].bitcast(I32),
-                    in_=scales[:, 4 * q:4 * q + 4, :].rearrange("a r n -> r a n").bitcast(I32),
-                )
-
-        nc.vector.memset(w_s[:].rearrange("p a n -> p (a n)").bitcast(I32), 0)
+        load_c(0)
         nc.sync.dma_start(offs_sb[:], offs)
-        for kind, q in LOADS:
-            if kind == "x":
-                load_x(q)
-            elif kind == "c":
-                load_c(q)
-            else:
-                load_half(wgt_sb, wgt, q)
-        if LATE_POS == 0:
-            nc.sync.dma_start(out=wgt_late[:], in_=wgt[:, HALF:J])
-        nc.sync.dma_start(out=wt_w[:].bitcast(I32), in_=wt_words.rearrange("a p n i -> p a (n i)").bitcast(I32))
-        load_scales(2, wx_scales)
-        nc.sync.dma_start(out=wx_w[:].bitcast(I32), in_=wx_words[0].rearrange("p n i -> p (n i)").bitcast(I32))
-        load_scales(0, wt_scales)
+        load_half(wgt_sb, wgt, 0)
+        load_x(0)
+        load_half(wgt_sb, wgt, 1)
+        for q in range(1, 6):
+            load_x(q)
+        load_c(1)
+        load_x(6)
+        load_x(7)
         with nc.allow_non_contiguous_dma(reason="one bias value to a partition and output tile"):
             nc.sync.dma_start(out=bias[:], in_=b.rearrange("(m p) -> p m", p=P))
+        nc.sync.dma_start(out=wt_w[:].bitcast(I32), in_=wt_words.rearrange("a p n i -> p a (n i)").bitcast(I32))
+        nc.sync.dma_start(out=wx_w[:].bitcast(I32), in_=wx_words[0].rearrange("p n i -> p (n i)").bitcast(I32))
         nc.sync.dma_start(offs2_sb[:], offs2)
         load_half(wgo_sb, wgo, 0)
-        if LATE_POS == 1:
-            nc.sync.dma_start(out=wgt_late[:], in_=wgt[:, HALF:J])
         load_half(wgo_sb, wgo, 1)
-        if LATE_POS == 2:
-            nc.sync.dma_start(out=wgt_late[:], in_=wgt[:, HALF:J])
 
         make_identity(nc, eye[:])
-
         nc.vector.memset(eye4[:].bitcast(I32), 0)
         nc.scalar.copy(
             out=eye4[:].rearrange("p (t x) -> p t x", t=PACK)[:, :, 0:L:PACK],
             in_=eye[:].unsqueeze(1).to_broadcast([P, PACK, P]),
         )
-        for w in range(2):
-            nc.vector.memset(win[w][:], 0.0)
+        for m in range(ROW_TILES):
+            nc.vector.memset(win[m][:], 0.0)
         nc.vector.quantize_mx(out=eye_w[:].bitcast(FP8X4), scales=eye_s[:], in_=eye4[:, 0:PACK * L])
 
-        def by_fours_src(ap):
-            return ap.rearrange("p t (g e) -> p g t e", e=2)
-
-        def by_fours_dst(ap):
-            return ap.rearrange("p (g e t) -> p g t e", e=2, t=PACK)
-
-        def interleave(src, z=None, on_vector=False):
-            if z is None:
-                z = ring.tile([P, PACK * CH], BF16, name="z", tag="z", bufs=6, align_bytes=64)
-            copy = nc.vector.tensor_copy if on_vector else nc.scalar.copy
-            copy(out=by_fours_dst(z[:]), in_=by_fours_src(src))
+        def interleave(name, src, tag=None):
+            z = sb(name, [P, PACK * src.shape[2]], BF16, tag)
+            nc.scalar.copy(
+                out=z[:].rearrange("p (g e t) -> p g t e", e=2, t=PACK),
+                in_=src.rearrange("p t (g e) -> p g t e", e=2),
+            )
             return z
 
-        def quantise(z, h, o, j0):
-            cols = slice(j0, j0 + z.shape[1] // PACK)
-            nc.vector.quantize_mx(out=act_w[h][o][:, cols].bitcast(FP8X4), scales=act_s[h][o][:, cols], in_=z[:])
+        def operand(name, cols, tag=None):
+            return sb(name + "_w", [P, cols], U32, tag), sb(name + "_s", [P, cols], U8)
 
-        def tier_one(u):
-            quantise(interleave(c_sb[u][:], on_vector=u in ZV), u // 2, 2, (u % 2) * CH)
+        def quantise(op, cols, z):
+            nc.vector.quantize_mx(out=op[0][:, cols].bitcast(FP8X4), scales=op[1][:, cols], in_=z[:])
 
-        turned = {}
-
-        def turn_c(u):
-            for s in range(CH // DQ):
-                bank = psum.tile([P, PACK, P], F32, name="turn", tag=TURN[0], bufs=TURN[1])
-                for t in range(PACK):
-                    nc.tensor.transpose(bank[:, t, :], c_sb[u][:, t, s * DQ:(s + 1) * DQ], eye[:])
-                ct = ring.tile([P, PACK, P], F32, name="ct", tag="ct", bufs=CTB)
-                nc.scalar.copy(out=ct[:], in_=bank[:])
-                turned[u, s] = ct
-
-        def residual(u):
-            h, j0 = u // 2, (u % 2) * CH
-            r = r_half[h][:, PACK * j0:PACK * (j0 + CH)]
-            for s in range(CH // DQ):
-                cols = slice(j0 + s * DQ, j0 + (s + 1) * DQ)
-                dq = psum.tile([P, L], F32, name="dq", tag="dq", bufs=DQB)
+        def negated_values(h, cq, banks):
+            nq = sb("nq%d" % h, [P, PACK, HALF], F32, "nq")
+            for t in range(PACK):
+                dq = bank("dq%d%d" % (h, t), banks[t])
                 nc.tensor.matmul_mx(
                     out=dq[:],
-                    lhsT=act_w[h][2][:, cols].bitcast(FP8X4),
-                    lhsT_scale=act_s[h][2][:, cols],
-                    rhs=eye_w[:].bitcast(FP8X4),
-                    rhs_scale=eye_s[:],
+                    lhsT=eye_w[:, t * P:(t + 1) * P].bitcast(FP8X4),
+                    lhsT_scale=eye_s[:, t * P:(t + 1) * P],
+                    rhs=cq[0][:].bitcast(FP8X4),
+                    rhs_scale=cq[1][:],
                     start=True,
                     stop=True,
                 )
-                nq = ring.tile([P, L], F32, name="nq", tag="nq", bufs=NQB)
-                nc.scalar.activation(out=nq[:], in_=dq[:], func=COPY, scale=-1.0)
-                diff = psum.tile([P, PACK, DQ], F32, name="diff", tag="diff", bufs=DIFFB)
-                if EARLY:
-                    for t in range(PACK):
-                        nc.tensor.matmul(diff[:, t, :], lhsT=turned[u, s][:, t, :], rhs=eye[:], start=(t == 0), stop=False, is_transpose=True)
-                    for t in range(PACK):
-                        nc.tensor.matmul(diff[:, t, :], lhsT=nq[:, t * P:(t + 1) * P], rhs=eye[:], start=False, stop=(t == PACK - 1), is_transpose=True)
-                else:
-                    for t in range(PACK):
-                        nc.tensor.matmul(diff[:, t, :], lhsT=turned[u, s][:, t, :], rhs=eye[:], start=True, stop=False, is_transpose=True)
-                        nc.tensor.matmul(diff[:, t, :], lhsT=nq[:, t * P:(t + 1) * P], rhs=eye[:], start=False, stop=True, is_transpose=True)
-                nc.scalar.copy(
-                    out=by_fours_dst(r[:, s * PACK * DQ:(s + 1) * PACK * DQ]),
-                    in_=by_fours_src(diff[:]),
-                )
+                nc.scalar.activation(out=nq[:, t, :], in_=dq[:], func=COPY, scale=-1.0)
+            return nq
 
-        def residual_on_vector(u):
-            h, j0 = u // 2, (u % 2) * CH
-            r = r_half[h][:, PACK * j0:PACK * (j0 + CH)]
-            for s in range(CH // DQ):
-                dq = psum.tile([P, PACK, DQ], F32, name="dq", tag="dq", bufs=DQB)
-                cols = slice(j0 + s * DQ, j0 + (s + 1) * DQ)
+        def turned_residual(h, s, nq, n):
+            cols = slice(s * P, (s + 1) * P)
+            diff = bank("diff%d%d" % (h, s), n)
+            for term, src in enumerate((c_sb[h], nq)):
                 for t in range(PACK):
-                    nc.tensor.matmul_mx(
-                        out=dq[:, t, :],
-                        lhsT=eye_w[:, t * P:(t + 1) * P].bitcast(FP8X4),
-                        lhsT_scale=eye_s[:, t * P:(t + 1) * P],
-                        rhs=act_w[h][2][:, cols].bitcast(FP8X4),
-                        rhs_scale=act_s[h][2][:, cols],
-                        start=True,
-                        stop=True,
+                    nc.tensor.matmul(
+                        diff[:, t * P:(t + 1) * P],
+                        lhsT=src[:, t, cols],
+                        rhs=eye[:],
+                        start=(term == 0 and t == 0),
+                        stop=(term == 1 and t == PACK - 1),
+                        is_transpose=True,
                     )
-                nc.vector.tensor_tensor(
-                    by_fours_dst(r[:, s * PACK * DQ:(s + 1) * PACK * DQ]),
-                    by_fours_src(c_sb[u][:, :, s * DQ:(s + 1) * DQ]),
-                    by_fours_src(dq[:]),
-                    SUB,
+            rt = sb("rt%d%d" % (h, s), [P, L], BF16, "rt%d" % s)
+            nc.scalar.copy(
+                out=rt[:].rearrange("j (u p e) -> j u p e", u=2, e=2),
+                in_=diff[:].rearrange("j (u e p) -> j u p e", u=2, e=2),
+            )
+            return rt
+
+        def turn_back(h, pair, rts, r, n):
+            back = bank("back%d%d" % (h, pair), n)
+            for s in range(2):
+                words = rts[s][:].bitcast(F32)
+                for u in range(2):
+                    at = (2 * s + u) * P
+                    nc.tensor.transpose(back[:, at:at + P], words[:, u * P:(u + 1) * P], eye[:])
+            nc.scalar.copy(
+                out=r[:].bitcast(F32)[:, pair * BANK:(pair + 1) * BANK].rearrange("p (s j u) -> p s j u", s=2, u=2),
+                in_=back[:].rearrange("p (s u j) -> p s j u", s=2, u=2),
+            )
+
+        def gather(g, q, cols):
+            at = (q % PACK) * J
+            nc.vector.tensor_tensor(
+                g[:, at + cols.start:at + cols.stop],
+                x_sb[q][:].indirect(offs_sb[:, list_cols(cols)]),
+                wgt_sb[:, cols],
+                MULT,
+            )
+
+        def planes(g, cols):
+            return g[:].rearrange("p (t j) -> p t j", t=PACK)[:, :, cols]
+
+        def project(name, m, cols, passes, n, tag=None):
+            acc = bank("acc" + name, n)[:, 0:width(cols)]
+            rows = slice(m * P, (m + 1) * P)
+            for i, (a, op, at) in enumerate(passes):
+                words = wt_w[:, a, rows] if a < 2 else wx_w[:, rows]
+                nc.tensor.matmul_mx(
+                    out=acc,
+                    lhsT=words.bitcast(FP8X4),
+                    lhsT_scale=w_s[:, a, rows],
+                    rhs=op[0][:, at].bitcast(FP8X4),
+                    rhs_scale=op[1][:, at],
+                    start=(i == 0),
+                    stop=(i == len(passes) - 1),
+                )
+            y = sb("y" + name, [P, width(cols)], F32, tag)
+            nc.scalar.activation(out=y[:], in_=acc, func=IDENT, bias=bias[:, m:m + 1])
+            return y
+
+        def scatter(m, cols, y):
+            nc.vector.tensor_tensor(win[m][:].indirect(offs2_sb[:, list_cols(cols)]), y[:], wgo_sb[:, cols], MULT)
+
+        whole = slice(0, HALF)
+
+        cq0 = operand("cq0", HALF)
+        for name, cols in (("zca", A), ("zcb", B)):
+            quantise(cq0, cols, interleave(name, c_sb[0][:, :, cols]))
+
+        w_s = sb("w_s", [P, 3, N], U8, "zcb")
+        nc.gpsimd.memset(w_s[:].rearrange("p a n -> p (a n)").bitcast(I32), 0)
+        for first, scales in ((2, wx_scales), (0, wt_scales)):
+            for q in range(4):
+                nc.gpsimd.dma_start(
+                    out=w_s[32 * q:32 * q + 4, first:first + scales.shape[0], :].bitcast(I32),
+                    in_=scales[:, 4 * q:4 * q + 4, :].rearrange("a r n -> r a n").bitcast(I32),
                 )
 
-        def tier_two(u):
-            h, j0 = u // 2, (u % 2) * CH
-            if not MERGE[h]:
-                quantise(r_half[h][:, PACK * j0:PACK * (j0 + CH)], h, 3, j0)
-            elif j0:
-                quantise(r_half[h], h, 3, 0)
+        g0 = sb("g0", [P, PACK * J], F32)
+        gather(g0, 0, whole)
+        gather(g0, 0, C)
+        nq = negated_values(0, cq0, (4, 5, 4, 5))
+        rts = [turned_residual(0, s, nq, n) for s, n in enumerate((6, 7, 0, 1))]
+        r0 = sb("r0", [P, PACK * HALF], BF16)
+        for pair in range(2):
+            turn_back(0, pair, rts[2 * pair:2 * pair + 2], r0, 2 + pair)
+        cr0 = operand("cr0", HALF)
+        quantise(cr0, whole, r0)
+        for q in range(1, 4):
+            gather(g0, q, slice(0, J))
 
-        def gather(q, h):
-            cols = slice(h * HALF // 16, (h + 1) * HALF // 16)
-            nc.vector.tensor_tensor(
-                gath[q // PACK][h][:, q % PACK, :], x_sb[q][:].indirect(offs_sb[:, cols]), (wgt_late if h == 1 and q >= LATE_FROM else wgt_sb[h])[:], MULT
-            )
+        xq0 = [operand("xq0%d" % h, HALF) for h in range(2)]
+        g1 = sb("g1", [P, PACK * J], F32, "x0")
+        gather(g1, 4, slice(0, J))
+        quantise(xq0[0], whole, interleave("z00", planes(g0, whole)))
+        gather(g1, 5, slice(0, J))
+        quantise(xq0[1], whole, interleave("z01", planes(g0, C)))
+        gather(g1, 6, slice(0, J))
+        zc1 = interleave("zc1", c_sb[1][:])
+        for cols in (A, B, C):
+            gather(g1, 7, cols)
 
-        zs = {}
+        xq1a = operand("xq1a", QUARTER)
+        xq1b = operand("xq1b", QUARTER)
+        quantise(xq1a, A, interleave("z1a", planes(g1, A)))
+        cq1 = operand("cq1", HALF, "z1a")
+        quantise(cq1, whole, zc1)
+        quantise(xq1b, A, interleave("z1b", planes(g1, B)))
 
-        def x_interleave(a, h):
-            for s in range(HALF // CH):
-                zs[a, h, s] = interleave(gath[a][h][:, :, s * CH:(s + 1) * CH])
+        passes_a = ((2, cq0, A), (2, cr0, A), (0, xq0[0], A), (1, xq1a, A))
+        passes_b = ((2, cq0, B), (2, cr0, B), (0, xq0[0], B), (1, xq1b, A))
+        ya = [project("a%d" % m, m, A, passes_a, m) for m in range(ROW_TILES)]
+        for m in range(ROW_TILES):
+            scatter(m, A, ya[m])
 
-        def x_quantise(a, h, s):
-            quantise(zs[a, h, s], h, a, s * CH)
+        nq = negated_values(1, cq1, (4, 5, 4, 5))
+        xq1c = operand("xq1c", HALF)
+        quantise(xq1c, whole, interleave("z1c", planes(g1, C), "eye_w"))
+        scatter(0, B, project("b0", 0, B, passes_b, 5))
+        rts = [turned_residual(1, s, nq, n) for s, n in enumerate((6, 7, 0, 1))]
+        scatter(1, B, project("b1", 1, B, passes_b, 7))
+        scatter(2, B, project("b2", 2, B, passes_b, 1))
+        r1 = sb("r1", [P, PACK * HALF], BF16, "r0")
+        for pair in range(2):
+            turn_back(1, pair, rts[2 * pair:2 * pair + 2], r1, 2 + pair)
+        cr1 = operand("cr1", HALF)
+        quantise(cr1, whole, r1)
+        scatter(3, B, project("b3", 3, B, passes_b, 3))
 
-        acc = {}
-        order = (2, 3, 0, 1)
-
-        def product(m, h, o):
-            if o == order[0]:
-                acc[m, h] = psum.tile([P, HALF], F32, name="acc", tag="acc", bufs=ACCB)
-            cols = slice(m * P, (m + 1) * P)
-            words = wt_w[:, o, cols] if o < 2 else wx_w[:, cols]
-            nc.tensor.matmul_mx(
-                out=acc[m, h][:],
-                lhsT=words.bitcast(FP8X4),
-                lhsT_scale=w_s[:, min(o, 2), cols],
-                rhs=act_w[h][o][:].bitcast(FP8X4),
-                rhs_scale=act_s[h][o][:],
-                start=(o == order[0]),
-                stop=(o == order[-1]),
-            )
-
-        ys = {}
-
-        def finish(m, h):
-            product(m, h, order[-1])
-            empty(m, h)
-
-        def empty(m, h):
-            y = y_first[m] if h == 0 and m < 2 else ring.tile([P, HALF], F32, name="y", tag="y", bufs=6)
-            nc.scalar.activation(out=y[:], in_=acc[m, h][:], func=IDENT, bias=bias[:, m:m + 1])
-            ys[m, h] = y
-
-        def scatter(m, h):
-            cols = slice(h * HALF // 16, (h + 1) * HALF // 16)
-            nc.vector.tensor_tensor(win[m][:].indirect(offs2_sb[:, cols]), ys[m, h][:], wgo_sb[h][:], MULT)
-
-        def store(m):
+        passes_c = ((2, cq1, whole), (0, xq0[1], whole), (2, cr1, whole), (1, xq1c, whole))
+        for m, n in enumerate((4, 6, 0, 2)):
+            scatter(m, C, project("c%d" % m, m, C, passes_c, n, "x%d" % (m + 1)))
             nc.sync.dma_start(out=out[m * P:(m + 1) * P, :], in_=win[m][:])
-
-        def chunk(u):
-            tier_one(u)
-            if u in VEC:
-                residual_on_vector(u)
-            else:
-                turn_c(u)
-                residual(u)
-            tier_two(u)
-
-        chunk(0)
-        for q in range(4):
-            gather(q, 0)
-            if q == 3 and W00:
-                z_wide = keep.tile([P, PACK * HALF], BF16, name="z_wide", align_bytes=64)
-                interleave(gath[0][0][:], z_wide)
-                quantise(z_wide, 0, 0, 0)
-            elif q == 3:
-                x_interleave(0, 0)
-                x_quantise(0, 0, 0)
-                x_quantise(0, 0, 1)
-            gather(q, 1)
-            if q > 0:
-                chunk(q)
-        for q in range(4, 8):
-            gather(q, 0)
-        x_interleave(1, 0)
-        for m in range(ACCB):
-            for o in order[:-1]:
-                product(m, 0, o)
-        x_quantise(1, 0, 0)
-        x_quantise(1, 0, 1)
-        for q in range(4, 8):
-            gather(q, 1)
-        for m in range(4):
-            if m >= ACCB:
-                for o in order[:-1]:
-                    product(m, 0, o)
-            finish(m, 0)
-        if HOLD01:
-            z_first = keep.tile([P, PACK * HALF], BF16, name="z_first", tag="as02", align_bytes=64)
-            interleave(gath[0][1][:], z_first)
-            quantise(z_first, 1, 0, 0)
-        elif W01:
-            z_first = keep.tile([P, PACK * HALF], BF16, name="z_first", align_bytes=64)
-            interleave(gath[0][1][:], z_first)
-            quantise(z_first, 1, 0, 0)
-        else:
-            x_interleave(0, 1)
-            x_quantise(0, 1, 0)
-            x_quantise(0, 1, 1)
-        z_last = keep.tile([P, PACK * HALF], BF16, name="z_last", tag="aw02", align_bytes=64)
-        interleave(gath[1][1][:], z_last)
-        quantise(z_last, 1, 1, 0)
-        for m in range(4):
-            for o in order[:-1]:
-                product(m, 1, o)
-            finish(m, 1)
-        for m in range(4):
-            if m >= 2:
-                for s in range(MSP):
-                    nc.gpsimd.memset(win[m][:, s * T // MSP:(s + 1) * T // MSP], 0.0)
-            scatter(m, 0)
-        for m in range(4):
-            scatter(m, 1)
-            store(m)

@@ -83,16 +83,25 @@ def tile_list_scatb_kernel(
             load_x(q)
         load_c(1)
         load_x(6)
-        load_x(7)
-        with nc.allow_non_contiguous_dma(reason="one bias value to a partition and output tile"):
-            nc.sync.dma_start(out=bias[:], in_=b.rearrange("(m p) -> p m", p=P))
-        nc.sync.dma_start(out=wt_w[:].bitcast(I32), in_=wt_words.rearrange("a p n i -> p a (n i)").bitcast(I32))
         nc.sync.dma_start(out=wx_w[:].bitcast(I32), in_=wx_words[0].rearrange("p n i -> p (n i)").bitcast(I32))
+        load_x(7)
+        nc.sync.dma_start(out=wt_w[:].bitcast(I32), in_=wt_words.rearrange("a p n i -> p a (n i)").bitcast(I32))
         nc.sync.dma_start(offs2_sb[:], offs2)
         load_half(wgo_sb, wgo, 0)
         load_half(wgo_sb, wgo, 1)
 
         make_identity(nc, eye[:])
+        b_rows = sb("b_rows", [P, P], F32)
+        nc.gpsimd.memset(b_rows[:], 0.0)
+        w_s = sb("w_s", [P, 3, N], U8)
+        nc.gpsimd.memset(w_s[:].rearrange("p a n -> p (a n)").bitcast(I32), 0)
+        nc.gpsimd.dma_start(out=b_rows[0:ROW_TILES, :], in_=b.rearrange("(m p) -> m p", p=P))
+        for first, scales in ((2, wx_scales), (0, wt_scales)):
+            for q in range(4):
+                nc.gpsimd.dma_start(
+                    out=w_s[32 * q:32 * q + 4, first:first + scales.shape[0], :].bitcast(I32),
+                    in_=scales[:, 4 * q:4 * q + 4, :].rearrange("a r n -> r a n").bitcast(I32),
+                )
         nc.vector.memset(eye4[:].bitcast(I32), 0)
         nc.scalar.copy(
             out=eye4[:].rearrange("p (t x) -> p t x", t=PACK)[:, :, 0:L:PACK],
@@ -203,15 +212,6 @@ def tile_list_scatb_kernel(
         for name, cols in (("zca", A), ("zcb", B)):
             quantise(cq0, cols, interleave(name, c_sb[0][:, :, cols]))
 
-        w_s = sb("w_s", [P, 3, N], U8, "zcb")
-        nc.gpsimd.memset(w_s[:].rearrange("p a n -> p (a n)").bitcast(I32), 0)
-        for first, scales in ((2, wx_scales), (0, wt_scales)):
-            for q in range(4):
-                nc.gpsimd.dma_start(
-                    out=w_s[32 * q:32 * q + 4, first:first + scales.shape[0], :].bitcast(I32),
-                    in_=scales[:, 4 * q:4 * q + 4, :].rearrange("a r n -> r a n").bitcast(I32),
-                )
-
         g0 = sb("g0", [P, PACK * J], F32)
         gather(g0, 0, whole)
         gather(g0, 0, C)
@@ -220,18 +220,22 @@ def tile_list_scatb_kernel(
         r0 = sb("r0", [P, PACK * HALF], BF16)
         for pair in range(2):
             turn_back(0, pair, rts[2 * pair:2 * pair + 2], r0, 2 + pair)
-        cr0 = operand("cr0", HALF)
-        quantise(cr0, whole, r0)
+        b_cols = bank("b_cols", 4)
+        nc.tensor.transpose(b_cols[:, 0:P], b_rows[:], eye[:])
+        nc.scalar.copy(out=bias[:], in_=b_cols[:, 0:ROW_TILES])
         for q in range(1, 4):
             gather(g0, q, slice(0, J))
 
-        xq0 = [operand("xq0%d" % h, HALF) for h in range(2)]
         g1 = sb("g1", [P, PACK * J], F32, "x0")
         gather(g1, 4, slice(0, J))
-        quantise(xq0[0], whole, interleave("z00", planes(g0, whole)))
-        gather(g1, 5, slice(0, J))
-        quantise(xq0[1], whole, interleave("z01", planes(g0, C)))
-        gather(g1, 6, slice(0, J))
+        cr0 = operand("cr0", HALF, "x4")
+        quantise(cr0, whole, r0)
+        z0 = [interleave("z0%d" % h, planes(g0, cols)) for h, cols in enumerate((whole, C))]
+        xq0 = []
+        for h in range(2):
+            gather(g1, 5 + h, slice(0, J))
+            xq0.append(operand("xq0%d" % h, HALF, "x%d" % (5 + h)))
+            quantise(xq0[h], whole, z0[h])
         zc1 = interleave("zc1", c_sb[1][:])
         for cols in (A, B, C):
             gather(g1, 7, cols)
@@ -265,5 +269,5 @@ def tile_list_scatb_kernel(
 
         passes_c = ((2, cq1, whole), (0, xq0[1], whole), (2, cr1, whole), (1, xq1c, whole))
         for m, n in enumerate((4, 6, 0, 2)):
-            scatter(m, C, project("c%d" % m, m, C, passes_c, n, "x%d" % (m + 1)))
+            scatter(m, C, project("c%d" % m, m, C, passes_c, n, ("x1", "x2", "x3", "x7")[m]))
             nc.sync.dma_start(out=out[m * P:(m + 1) * P, :], in_=win[m][:])

@@ -84,10 +84,10 @@ def tile_list_scatb_kernel(
         load_c(1)
         load_x(6)
         nc.sync.dma_start(out=wx_w[:].bitcast(I32), in_=wx_words[0].rearrange("p n i -> p (n i)").bitcast(I32))
-        load_x(7)
         nc.sync.dma_start(out=wt_w[:].bitcast(I32), in_=wt_words.rearrange("a p n i -> p a (n i)").bitcast(I32))
         nc.sync.dma_start(offs2_sb[:], offs2)
         load_half(wgo_sb, wgo, 0)
+        load_x(7)
         load_half(wgo_sb, wgo, 1)
 
         make_identity(nc, eye[:])

@@ -74,20 +74,22 @@ def tile_list_scatb_kernel(
         def load_half(tile, src, h):
             nc.sync.dma_start(out=tile[:, h * HALF:(h + 1) * HALF], in_=src[:, h * HALF:(h + 1) * HALF])
 
+        def load_wt(a):
+            nc.sync.dma_start(out=wt_w[:, a, :].bitcast(I32), in_=wt_words[a].rearrange("p n i -> p (n i)").bitcast(I32))
+
         load_c(0)
         nc.sync.dma_start(offs_sb[:], offs)
-        load_half(wgt_sb, wgt, 0)
-        load_x(0)
-        load_half(wgt_sb, wgt, 1)
-        for q in range(1, 6):
+        nc.sync.dma_start(out=wgt_sb[:], in_=wgt)
+        for q in range(6):
             load_x(q)
         load_c(1)
         load_x(6)
         nc.sync.dma_start(out=wx_w[:].bitcast(I32), in_=wx_words[0].rearrange("p n i -> p (n i)").bitcast(I32))
-        nc.sync.dma_start(out=wt_w[:].bitcast(I32), in_=wt_words.rearrange("a p n i -> p a (n i)").bitcast(I32))
+        load_wt(0)
+        load_x(7)
+        load_wt(1)
         nc.sync.dma_start(offs2_sb[:], offs2)
         load_half(wgo_sb, wgo, 0)
-        load_x(7)
         load_half(wgo_sb, wgo, 1)
 
         make_identity(nc, eye[:])
@@ -108,15 +110,18 @@ def tile_list_scatb_kernel(
             in_=eye[:].unsqueeze(1).to_broadcast([P, PACK, P]),
         )
         for m in range(ROW_TILES):
-            nc.vector.memset(win[m][:], 0.0)
+            nc.vector.memset(win[m][:].bitcast(I32), 0)
         nc.vector.quantize_mx(out=eye_w[:].bitcast(FP8X4), scales=eye_s[:], in_=eye4[:, 0:PACK * L])
+
+        def interleave_into(z, src):
+            nc.scalar.copy(
+                out=z.rearrange("p (g e t) -> p g t e", e=2, t=PACK),
+                in_=src.rearrange("p t (g e) -> p g t e", e=2),
+            )
 
         def interleave(name, src, tag=None):
             z = sb(name, [P, PACK * src.shape[2]], BF16, tag)
-            nc.scalar.copy(
-                out=z[:].rearrange("p (g e t) -> p g t e", e=2, t=PACK),
-                in_=src.rearrange("p t (g e) -> p g t e", e=2),
-            )
+            interleave_into(z[:], src)
             return z
 
         def operand(name, cols, tag=None):
@@ -209,12 +214,10 @@ def tile_list_scatb_kernel(
         whole = slice(0, HALF)
 
         cq0 = operand("cq0", HALF)
-        for name, cols in (("zca", A), ("zcb", B)):
-            quantise(cq0, cols, interleave(name, c_sb[0][:, :, cols]))
+        quantise(cq0, whole, interleave("zc0", c_sb[0][:]))
 
         g0 = sb("g0", [P, PACK * J], F32)
-        gather(g0, 0, whole)
-        gather(g0, 0, C)
+        gather(g0, 0, slice(0, J))
         nq = negated_values(0, cq0, (4, 5, 4, 5))
         rts = [turned_residual(0, s, nq, n) for s, n in enumerate((6, 7, 0, 1))]
         r0 = sb("r0", [P, PACK * HALF], BF16)
@@ -230,44 +233,44 @@ def tile_list_scatb_kernel(
         gather(g1, 4, slice(0, J))
         cr0 = operand("cr0", HALF, "x4")
         quantise(cr0, whole, r0)
-        z0 = [interleave("z0%d" % h, planes(g0, cols)) for h, cols in enumerate((whole, C))]
-        xq0 = []
-        for h in range(2):
-            gather(g1, 5 + h, slice(0, J))
-            xq0.append(operand("xq0%d" % h, HALF, "x%d" % (5 + h)))
-            quantise(xq0[h], whole, z0[h])
+        z0 = sb("z0", [P, PACK * J], BF16)
+        for cols in (whole, C):
+            interleave_into(z0[:, PACK * cols.start:PACK * cols.stop], planes(g0, cols))
+        gather(g1, 5, slice(0, J))
+        xq0 = operand("xq0", J)
+        quantise(xq0, slice(0, J), z0)
+        gather(g1, 6, slice(0, J))
         zc1 = interleave("zc1", c_sb[1][:])
         for cols in (A, B, C):
             gather(g1, 7, cols)
 
-        xq1a = operand("xq1a", QUARTER)
-        xq1b = operand("xq1b", QUARTER)
-        quantise(xq1a, A, interleave("z1a", planes(g1, A)))
+        xq1 = operand("xq1", HALF)
+        quantise(xq1, A, interleave("z1a", planes(g1, A)))
         cq1 = operand("cq1", HALF, "z1a")
         quantise(cq1, whole, zc1)
-        quantise(xq1b, A, interleave("z1b", planes(g1, B)))
+        quantise(xq1, B, interleave("z1b", planes(g1, B)))
 
-        passes_a = ((2, cq0, A), (2, cr0, A), (0, xq0[0], A), (1, xq1a, A))
-        passes_b = ((2, cq0, B), (2, cr0, B), (0, xq0[0], B), (1, xq1b, A))
-        ya = [project("a%d" % m, m, A, passes_a, m) for m in range(ROW_TILES)]
-        for m in range(ROW_TILES):
-            scatter(m, A, ya[m])
+        def first_half(cols):
+            return ((2, cq0, cols), (2, cr0, cols), (0, xq0, cols), (1, xq1, cols))
 
-        nq = negated_values(1, cq1, (4, 5, 4, 5))
+        for m in (0, 1):
+            scatter(m, A, project("a%d" % m, m, A, first_half(A), m))
         xq1c = operand("xq1c", HALF)
-        quantise(xq1c, whole, interleave("z1c", planes(g1, C), "eye_w"))
-        scatter(0, B, project("b0", 0, B, passes_b, 5))
-        rts = [turned_residual(1, s, nq, n) for s, n in enumerate((6, 7, 0, 1))]
-        scatter(1, B, project("b1", 1, B, passes_b, 7))
-        scatter(2, B, project("b2", 2, B, passes_b, 1))
+        quantise(xq1c, whole, interleave("z1c", planes(g1, C), "z1b"))
+        for m in (2, 3):
+            scatter(m, whole, project("ab%d" % m, m, whole, first_half(whole), m))
+        nq = negated_values(1, cq1, (0, 1, 2, 3))
+        rts = [turned_residual(1, s, nq, 4 + s) for s in range(4)]
+        scatter(0, B, project("b0", 0, B, first_half(B), 3))
         r1 = sb("r1", [P, PACK * HALF], BF16, "r0")
-        for pair in range(2):
-            turn_back(1, pair, rts[2 * pair:2 * pair + 2], r1, 2 + pair)
+        for pair, n in enumerate((1, 2)):
+            turn_back(1, pair, rts[2 * pair:2 * pair + 2], r1, n)
         cr1 = operand("cr1", HALF)
         quantise(cr1, whole, r1)
-        scatter(3, B, project("b3", 3, B, passes_b, 3))
+        scatter(1, B, project("b1", 1, B, first_half(B), 7))
 
-        passes_c = ((2, cq1, whole), (0, xq0[1], whole), (2, cr1, whole), (1, xq1c, whole))
-        for m, n in enumerate((4, 6, 0, 2)):
-            scatter(m, C, project("c%d" % m, m, C, passes_c, n, ("x1", "x2", "x3", "x7")[m]))
+        second_half = ((2, cq1, whole), (0, xq0, C), (1, xq1c, whole), (2, cr1, whole))
+        for m, n in enumerate((4, 2, 4, 2)):
+            passes = second_half[::-1] if m == 1 else second_half
+            scatter(m, C, project("c%d" % m, m, C, passes, n, ("x1", "x2", "x3", "x7")[m]))
             nc.sync.dma_start(out=out[m * P:(m + 1) * P, :], in_=win[m][:])

@@ -77,6 +77,14 @@ def tile_list_scatb_kernel(
         def load_wt(a):
             nc.sync.dma_start(out=wt_w[:, a, :].bitcast(I32), in_=wt_words[a].rearrange("p n i -> p (n i)").bitcast(I32))
 
+        def load_scales(plane, scales):
+            nc.gpsimd.memset(plane[:].rearrange("p a n -> p (a n)").bitcast(I32), 0)
+            for q in range(4):
+                nc.gpsimd.dma_start(
+                    out=plane[32 * q:32 * q + 4, :, :].bitcast(I32),
+                    in_=scales[:, 4 * q:4 * q + 4, :].rearrange("a r n -> r a n").bitcast(I32),
+                )
+
         load_c(0)
         nc.sync.dma_start(offs_sb[:], offs)
         nc.sync.dma_start(out=wgt_sb[:], in_=wgt)
@@ -85,8 +93,8 @@ def tile_list_scatb_kernel(
         load_c(1)
         load_x(6)
         nc.sync.dma_start(out=wx_w[:].bitcast(I32), in_=wx_words[0].rearrange("p n i -> p (n i)").bitcast(I32))
-        load_wt(0)
         load_x(7)
+        load_wt(0)
         load_wt(1)
         nc.sync.dma_start(offs2_sb[:], offs2)
         load_half(wgo_sb, wgo, 0)
@@ -95,15 +103,9 @@ def tile_list_scatb_kernel(
         make_identity(nc, eye[:])
         b_rows = sb("b_rows", [P, P], F32)
         nc.gpsimd.memset(b_rows[:], 0.0)
-        w_s = sb("w_s", [P, 3, N], U8)
-        nc.gpsimd.memset(w_s[:].rearrange("p a n -> p (a n)").bitcast(I32), 0)
         nc.gpsimd.dma_start(out=b_rows[0:ROW_TILES, :], in_=b.rearrange("(m p) -> m p", p=P))
-        for first, scales in ((2, wx_scales), (0, wt_scales)):
-            for q in range(4):
-                nc.gpsimd.dma_start(
-                    out=w_s[32 * q:32 * q + 4, first:first + scales.shape[0], :].bitcast(I32),
-                    in_=scales[:, 4 * q:4 * q + 4, :].rearrange("a r n -> r a n").bitcast(I32),
-                )
+        wx_s = sb("wx_s", [P, 1, N], U8)
+        load_scales(wx_s, wx_scales)
         nc.vector.memset(eye4[:].bitcast(I32), 0)
         nc.scalar.copy(
             out=eye4[:].rearrange("p (t x) -> p t x", t=PACK)[:, :, 0:L:PACK],
@@ -115,8 +117,8 @@ def tile_list_scatb_kernel(
 
         def interleave_into(z, src):
             nc.scalar.copy(
-                out=z.rearrange("p (g e t) -> p g t e", e=2, t=PACK),
-                in_=src.rearrange("p t (g e) -> p g t e", e=2),
+                out=z.rearrange("p (g e t) -> p g t e", e=4, t=PACK),
+                in_=src.rearrange("p t (g e) -> p g t e", e=4),
             )
 
         def interleave(name, src, tag=None):
@@ -161,8 +163,8 @@ def tile_list_scatb_kernel(
                     )
             rt = sb("rt%d%d" % (h, s), [P, L], BF16, "rt%d" % s)
             nc.scalar.copy(
-                out=rt[:].rearrange("j (u p e) -> j u p e", u=2, e=2),
-                in_=diff[:].rearrange("j (u e p) -> j u p e", u=2, e=2),
+                out=rt[:].rearrange("j (u g i e) -> j u g e i", u=2, i=2, e=2),
+                in_=diff[:].rearrange("j (u e g i) -> j u g e i", u=2, e=2, i=2),
             )
             return rt
 
@@ -174,8 +176,8 @@ def tile_list_scatb_kernel(
                     at = (2 * s + u) * P
                     nc.tensor.transpose(back[:, at:at + P], words[:, u * P:(u + 1) * P], eye[:])
             nc.scalar.copy(
-                out=r[:].bitcast(F32)[:, pair * BANK:(pair + 1) * BANK].rearrange("p (s j u) -> p s j u", s=2, u=2),
-                in_=back[:].rearrange("p (s u j) -> p s j u", s=2, u=2),
+                out=r[:].bitcast(F32)[:, pair * BANK:(pair + 1) * BANK].rearrange("p (s g i u) -> p s g u i", s=2, i=2, u=2),
+                in_=back[:].rearrange("p (s u g i) -> p s g u i", s=2, u=2, i=2),
             )
 
         def gather(g, q, cols):
@@ -195,10 +197,11 @@ def tile_list_scatb_kernel(
             rows = slice(m * P, (m + 1) * P)
             for i, (a, op, at) in enumerate(passes):
                 words = wt_w[:, a, rows] if a < 2 else wx_w[:, rows]
+                plane = wt_s[:, a, rows] if a < 2 else wx_s[:, 0, rows]
                 nc.tensor.matmul_mx(
                     out=acc,
                     lhsT=words.bitcast(FP8X4),
-                    lhsT_scale=w_s[:, a, rows],
+                    lhsT_scale=plane,
                     rhs=op[0][:, at].bitcast(FP8X4),
                     rhs_scale=op[1][:, at],
                     start=(i == 0),
@@ -216,9 +219,12 @@ def tile_list_scatb_kernel(
         cq0 = operand("cq0", HALF)
         quantise(cq0, whole, interleave("zc0", c_sb[0][:]))
 
+        wt_s = sb("wt_s", [P, 2, N], U8, "zc0")
+        load_scales(wt_s, wt_scales)
+
         g0 = sb("g0", [P, PACK * J], F32)
         gather(g0, 0, slice(0, J))
-        nq = negated_values(0, cq0, (4, 5, 4, 5))
+        nq = negated_values(0, cq0, (2, 3, 4, 5))
         rts = [turned_residual(0, s, nq, n) for s, n in enumerate((6, 7, 0, 1))]
         r0 = sb("r0", [P, PACK * HALF], BF16)
         for pair in range(2):
@@ -273,4 +279,9 @@ def tile_list_scatb_kernel(
         for m, n in enumerate((4, 2, 4, 2)):
             passes = second_half[::-1] if m == 1 else second_half
             scatter(m, C, project("c%d" % m, m, C, passes, n, ("x1", "x2", "x3", "x7")[m]))
-            nc.sync.dma_start(out=out[m * P:(m + 1) * P, :], in_=win[m][:])
+            rows = slice(m * P, (m + 1) * P)
+            if m < ROW_TILES - 1:
+                nc.sync.dma_start(out=out[rows, :], in_=win[m][:])
+            else:
+                nc.sync.dma_start(out=out[rows, 0:T // 2], in_=win[m][:, 0:T // 2])
+                nc.scalar.dma_start(out=out[rows, T // 2:T], in_=win[m][:, T // 2:T])

@@ -1,7 +1,6 @@
 from contextlib import ExitStack
 
 import concourse.mybir as mybir
-from concourse.masks import make_identity
 
 K, L, N, T, J = 1024, 512, 512, 2048, 1024
 FLOPS = 2 * (K + 2 * L) * N * J + 2 * L * L * J
@@ -19,11 +18,15 @@ COPY = mybir.ActivationFunctionType.Copy
 
 P = 128
 PACK = 4
+BANK = 512
+GROUP = 16
+ROW_TILES = N // P
+WX = 2
 HALF = J // 2
 QUARTER = J // 4
-BANK = 512
-ROW_TILES = N // P
-A, B, C = slice(0, QUARTER), slice(QUARTER, HALF), slice(HALF, J)
+Q0, Q1, LATE = slice(0, QUARTER), slice(QUARTER, HALF), slice(HALF, J)
+EARLY, EVERY = slice(0, HALF), slice(0, J)
+OWN = slice(0, HALF)
 
 
 def tile_list_scatb_kernel(
@@ -33,10 +36,11 @@ def tile_list_scatb_kernel(
     with ExitStack() as ctx:
         lists = ctx.enter_context(tc.tile_pool(name="lists", bufs=1))
         keep = ctx.enter_context(tc.tile_pool(name="keep", bufs=1))
+        placed = ctx.enter_context(tc.tile_pool(name="placed", bufs=1))
         psum = ctx.enter_context(tc.psum_pool(name="psum", bufs=1))
 
-        def sb(name, shape, dtype, tag=None):
-            return keep.tile(shape, dtype, name=name, tag=tag or name, align_bytes=64)
+        def sb(name, shape, dtype, after=None):
+            return keep.tile(shape, dtype, name=name, tag=after or name, align_bytes=64)
 
         def bank(name, n):
             return psum.tile([P, BANK], F32, name=name, tag="bank%d" % n)
@@ -45,10 +49,10 @@ def tile_list_scatb_kernel(
             return cols.stop - cols.start
 
         def list_cols(cols):
-            return slice(cols.start // 16, cols.stop // 16)
+            return slice(cols.start // GROUP, cols.stop // GROUP)
 
-        offs_sb = lists.tile([P, J // 16], U16, name="offs_sb")
-        offs2_sb = lists.tile([P, J // 16], U16, name="offs2_sb")
+        offs_sb = lists.tile([P, J // GROUP], U16, name="offs_sb")
+        offs2_sb = lists.tile([P, J // GROUP], U16, name="offs2_sb")
         x_sb = [sb("x%d" % q, [P, T], F32) for q in range(2 * PACK)]
         c_sb = [sb("c%d" % h, [P, PACK, HALF], F32) for h in range(2)]
         wgt_sb = sb("wgt", [P, J], F32)
@@ -60,7 +64,7 @@ def tile_list_scatb_kernel(
         eye4 = sb("eye4", [P, PACK * (L + 1)], BF16)
         eye_w = sb("eye_w", [P, L], U32)
         eye_s = sb("eye_s", [P, L], U8)
-        win = [sb("win%d" % m, [P, T], F32) for m in range(ROW_TILES)]
+        win = [sb("win%d" % m, [P, T], F32) for m in range(2)]
 
         x_planes = xT.rearrange("(a p i) t -> a i p t", a=2, i=PACK)
         c_rows = c.rearrange("(p i) j -> p i j", i=PACK)
@@ -71,14 +75,10 @@ def tile_list_scatb_kernel(
         def load_c(h):
             nc.sync.dma_start(out=c_sb[h][:], in_=c_rows[:, :, h * HALF:(h + 1) * HALF])
 
-        def load_half(tile, src, h):
-            nc.sync.dma_start(out=tile[:, h * HALF:(h + 1) * HALF], in_=src[:, h * HALF:(h + 1) * HALF])
-
-        def load_wt(a):
-            nc.sync.dma_start(out=wt_w[:, a, :].bitcast(I32), in_=wt_words[a].rearrange("p n i -> p (n i)").bitcast(I32))
+        def load_words(tile, words):
+            nc.sync.dma_start(out=tile.bitcast(I32), in_=words.rearrange("p n i -> p (n i)").bitcast(I32))
 
         def load_scales(plane, scales):
-            nc.gpsimd.memset(plane[:].rearrange("p a n -> p (a n)").bitcast(I32), 0)
             for q in range(4):
                 nc.gpsimd.dma_start(
                     out=plane[32 * q:32 * q + 4, :, :].bitcast(I32),
@@ -90,28 +90,40 @@ def tile_list_scatb_kernel(
         nc.sync.dma_start(out=wgt_sb[:], in_=wgt)
         for q in range(6):
             load_x(q)
+        with nc.allow_non_contiguous_dma(reason="one bias value to a partition and row tile"):
+            nc.sync.dma_start(out=bias[:], in_=b.rearrange("(m p) -> p m", p=P))
         load_c(1)
         load_x(6)
-        nc.sync.dma_start(out=wx_w[:].bitcast(I32), in_=wx_words[0].rearrange("p n i -> p (n i)").bitcast(I32))
+        load_words(wx_w[:], wx_words[0])
         load_x(7)
-        load_wt(0)
-        load_wt(1)
+        for a in range(2):
+            load_words(wt_w[:, a, :], wt_words[a])
         nc.sync.dma_start(offs2_sb[:], offs2)
-        load_half(wgo_sb, wgo, 0)
-        load_half(wgo_sb, wgo, 1)
+        for cols in (EARLY, LATE):
+            nc.sync.dma_start(out=wgo_sb[:, cols], in_=wgo[:, cols])
 
-        make_identity(nc, eye[:])
-        b_rows = sb("b_rows", [P, P], F32)
-        nc.gpsimd.memset(b_rows[:], 0.0)
-        nc.gpsimd.dma_start(out=b_rows[0:ROW_TILES, :], in_=b.rearrange("(m p) -> m p", p=P))
-        wx_s = sb("wx_s", [P, 1, N], U8)
-        load_scales(wx_s, wx_scales)
+        window_bytes = 4 * T
+        zeros = placed.tile([P, P], F32, name="zeros", offset=window_bytes - 2 * P)
+        nc.gpsimd.memset(zeros[:], 0.0)
+        nc.gpsimd.affine_select(
+            out=eye[:],
+            in_=zeros[:],
+            compare_op=mybir.AluOpType.not_equal,
+            fill=1.0,
+            base=0,
+            pattern=[[-1, P]],
+            channel_multiplier=1,
+        )
+        for m in (2, 3):
+            win.append(placed.tile([P, T], F32, name="win%d" % m, offset=window_bytes * (m - 2)))
+            nc.gpsimd.memset(win[m][:].bitcast(I32), 0)
+
         nc.vector.memset(eye4[:].bitcast(I32), 0)
         nc.scalar.copy(
             out=eye4[:].rearrange("p (t x) -> p t x", t=PACK)[:, :, 0:L:PACK],
             in_=eye[:].unsqueeze(1).to_broadcast([P, PACK, P]),
         )
-        for m in range(ROW_TILES):
+        for m in range(2):
             nc.vector.memset(win[m][:].bitcast(I32), 0)
         nc.vector.quantize_mx(out=eye_w[:].bitcast(FP8X4), scales=eye_s[:], in_=eye4[:, 0:PACK * L])
 
@@ -121,13 +133,13 @@ def tile_list_scatb_kernel(
                 in_=src.rearrange("p t (g e) -> p g t e", e=4),
             )
 
-        def interleave(name, src, tag=None):
-            z = sb(name, [P, PACK * src.shape[2]], BF16, tag)
+        def interleave(name, src, after=None):
+            z = sb(name, [P, PACK * src.shape[2]], BF16, after)
             interleave_into(z[:], src)
             return z
 
-        def operand(name, cols, tag=None):
-            return sb(name + "_w", [P, cols], U32, tag), sb(name + "_s", [P, cols], U8)
+        def operand(name, cols, after=None):
+            return sb(name + "_w", [P, cols], U32, after), sb(name + "_s", [P, cols], U8)
 
         def quantise(op, cols, z):
             nc.vector.quantize_mx(out=op[0][:, cols].bitcast(FP8X4), scales=op[1][:, cols], in_=z[:])
@@ -171,12 +183,13 @@ def tile_list_scatb_kernel(
         def turn_back(h, pair, rts, r, n):
             back = bank("back%d%d" % (h, pair), n)
             for s in range(2):
-                words = rts[s][:].bitcast(F32)
+                words = rts[2 * pair + s][:].bitcast(F32)
                 for u in range(2):
                     at = (2 * s + u) * P
                     nc.tensor.transpose(back[:, at:at + P], words[:, u * P:(u + 1) * P], eye[:])
+            r_words = r[:].bitcast(F32)[:, pair * BANK:(pair + 1) * BANK]
             nc.scalar.copy(
-                out=r[:].bitcast(F32)[:, pair * BANK:(pair + 1) * BANK].rearrange("p (s g i u) -> p s g u i", s=2, i=2, u=2),
+                out=r_words.rearrange("p (s g i u) -> p s g u i", s=2, i=2, u=2),
                 in_=back[:].rearrange("p (s u g i) -> p s g u i", s=2, u=2, i=2),
             )
 
@@ -192,93 +205,92 @@ def tile_list_scatb_kernel(
         def planes(g, cols):
             return g[:].rearrange("p (t j) -> p t j", t=PACK)[:, :, cols]
 
-        def project(name, m, cols, passes, n, tag=None):
+        def project(name, m, cols, passes, n, after=None, shift=bias):
             acc = bank("acc" + name, n)[:, 0:width(cols)]
             rows = slice(m * P, (m + 1) * P)
             for i, (a, op, at) in enumerate(passes):
-                words = wt_w[:, a, rows] if a < 2 else wx_w[:, rows]
-                plane = wt_s[:, a, rows] if a < 2 else wx_s[:, 0, rows]
+                words = wx_w[:, rows] if a == WX else wt_w[:, a, rows]
                 nc.tensor.matmul_mx(
                     out=acc,
                     lhsT=words.bitcast(FP8X4),
-                    lhsT_scale=plane,
+                    lhsT_scale=w_s[:, a, rows],
                     rhs=op[0][:, at].bitcast(FP8X4),
                     rhs_scale=op[1][:, at],
                     start=(i == 0),
                     stop=(i == len(passes) - 1),
                 )
-            y = sb("y" + name, [P, width(cols)], F32, tag)
-            nc.scalar.activation(out=y[:], in_=acc, func=IDENT, bias=bias[:, m:m + 1])
+            y = sb("y" + name, [P, width(cols)], F32, after)
+            nc.scalar.activation(out=y[:], in_=acc, func=IDENT, bias=shift[:, m:m + 1])
             return y
 
         def scatter(m, cols, y):
             nc.vector.tensor_tensor(win[m][:].indirect(offs2_sb[:, list_cols(cols)]), y[:], wgo_sb[:, cols], MULT)
 
-        whole = slice(0, HALF)
-
         cq0 = operand("cq0", HALF)
-        quantise(cq0, whole, interleave("zc0", c_sb[0][:]))
+        quantise(cq0, EARLY, interleave("zc0", c_sb[0][:]))
 
-        wt_s = sb("wt_s", [P, 2, N], U8, "zc0")
-        load_scales(wt_s, wt_scales)
+        w_s = sb("w_s", [P, 3, N], U8, "zc0")
+        nc.gpsimd.memset(w_s[:].rearrange("p a n -> p (a n)").bitcast(I32), 0)
+        load_scales(w_s[:, WX:WX + 1, :], wx_scales)
+        load_scales(w_s[:, 0:WX, :], wt_scales)
 
         g0 = sb("g0", [P, PACK * J], F32)
-        gather(g0, 0, slice(0, J))
+        gather(g0, 0, EVERY)
         nq = negated_values(0, cq0, (2, 3, 4, 5))
         rts = [turned_residual(0, s, nq, n) for s, n in enumerate((6, 7, 0, 1))]
         r0 = sb("r0", [P, PACK * HALF], BF16)
         for pair in range(2):
-            turn_back(0, pair, rts[2 * pair:2 * pair + 2], r0, 2 + pair)
-        b_cols = bank("b_cols", 4)
-        nc.tensor.transpose(b_cols[:, 0:P], b_rows[:], eye[:])
-        nc.scalar.copy(out=bias[:], in_=b_cols[:, 0:ROW_TILES])
-        for q in range(1, 4):
-            gather(g0, q, slice(0, J))
+            turn_back(0, pair, rts, r0, 2 + pair)
+        for q in range(1, PACK):
+            gather(g0, q, EVERY)
 
         g1 = sb("g1", [P, PACK * J], F32, "x0")
-        gather(g1, 4, slice(0, J))
+        gather(g1, 4, EVERY)
         cr0 = operand("cr0", HALF, "x4")
-        quantise(cr0, whole, r0)
+        quantise(cr0, EARLY, r0)
         z0 = sb("z0", [P, PACK * J], BF16)
-        for cols in (whole, C):
+        for cols in (EARLY, LATE):
             interleave_into(z0[:, PACK * cols.start:PACK * cols.stop], planes(g0, cols))
-        gather(g1, 5, slice(0, J))
+        gather(g1, 5, EVERY)
         xq0 = operand("xq0", J)
-        quantise(xq0, slice(0, J), z0)
-        gather(g1, 6, slice(0, J))
+        quantise(xq0, EVERY, z0)
+        gather(g1, 6, EVERY)
         zc1 = interleave("zc1", c_sb[1][:])
-        for cols in (A, B, C):
+        bias_q0 = sb("bias_q0", [P, 2], F32)
+        nc.scalar.copy(out=bias_q0[:], in_=bias[:, 0:2])
+        for cols in (Q0, Q1, LATE):
             gather(g1, 7, cols)
 
         xq1 = operand("xq1", HALF)
-        quantise(xq1, A, interleave("z1a", planes(g1, A)))
-        cq1 = operand("cq1", HALF, "z1a")
-        quantise(cq1, whole, zc1)
-        quantise(xq1, B, interleave("z1b", planes(g1, B)))
+        quantise(xq1, Q0, interleave("z1q0", planes(g1, Q0)))
+        cq1 = operand("cq1", HALF, "z1q0")
+        quantise(cq1, OWN, zc1)
+        quantise(xq1, Q1, interleave("z1q1", planes(g1, Q1)))
 
-        def first_half(cols):
-            return ((2, cq0, cols), (2, cr0, cols), (0, xq0, cols), (1, xq1, cols))
+        def early_passes(cols):
+            return ((WX, cq0, cols), (WX, cr0, cols), (0, xq0, cols), (1, xq1, cols))
 
         for m in (0, 1):
-            scatter(m, A, project("a%d" % m, m, A, first_half(A), m))
-        xq1c = operand("xq1c", HALF)
-        quantise(xq1c, whole, interleave("z1c", planes(g1, C), "z1b"))
+            scatter(m, Q0, project("q0%d" % m, m, Q0, early_passes(Q0), m, None, bias_q0))
+        xq1_late = operand("xq1_late", HALF)
+        quantise(xq1_late, OWN, interleave("z1_late", planes(g1, LATE), "bias_q0"))
         for m in (2, 3):
-            scatter(m, whole, project("ab%d" % m, m, whole, first_half(whole), m))
-        nq = negated_values(1, cq1, (0, 1, 2, 3))
-        rts = [turned_residual(1, s, nq, 4 + s) for s in range(4)]
-        scatter(0, B, project("b0", 0, B, first_half(B), 3))
-        r1 = sb("r1", [P, PACK * HALF], BF16, "r0")
-        for pair, n in enumerate((1, 2)):
-            turn_back(1, pair, rts[2 * pair:2 * pair + 2], r1, n)
-        cr1 = operand("cr1", HALF)
-        quantise(cr1, whole, r1)
-        scatter(1, B, project("b1", 1, B, first_half(B), 7))
+            scatter(m, EARLY, project("early%d" % m, m, EARLY, early_passes(EARLY), m))
 
-        second_half = ((2, cq1, whole), (0, xq0, C), (1, xq1c, whole), (2, cr1, whole))
-        for m, n in enumerate((4, 2, 4, 2)):
-            passes = second_half[::-1] if m == 1 else second_half
-            scatter(m, C, project("c%d" % m, m, C, passes, n, ("x1", "x2", "x3", "x7")[m]))
+        nq = negated_values(1, cq1, range(PACK))
+        rts = [turned_residual(1, s, nq, PACK + s) for s in range(PACK)]
+        scatter(0, Q1, project("q10", 0, Q1, early_passes(Q1), 3))
+        r1 = sb("r1", [P, PACK * HALF], BF16, "r0")
+        for pair in range(2):
+            turn_back(1, pair, rts, r1, pair)
+        cr1 = operand("cr1", HALF)
+        quantise(cr1, OWN, r1)
+        scatter(1, Q1, project("q11", 1, Q1, early_passes(Q1), 7))
+
+        late_passes = ((WX, cq1, OWN), (0, xq0, LATE), (1, xq1_late, OWN), (WX, cr1, OWN))
+        for m, plane in enumerate(("x1", "x2", "x3", "x7")):
+            passes = late_passes[::-1] if m == 1 else late_passes
+            scatter(m, LATE, project("late%d" % m, m, LATE, passes, 1 if m % 2 else 4, plane))
             rows = slice(m * P, (m + 1) * P)
             if m < ROW_TILES - 1:
                 nc.sync.dma_start(out=out[rows, :], in_=win[m][:])

@@ -36,7 +36,6 @@ def tile_list_scatb_kernel(
     with ExitStack() as ctx:
         lists = ctx.enter_context(tc.tile_pool(name="lists", bufs=1))
         keep = ctx.enter_context(tc.tile_pool(name="keep", bufs=1))
-        placed = ctx.enter_context(tc.tile_pool(name="placed", bufs=1))
         psum = ctx.enter_context(tc.psum_pool(name="psum", bufs=1))
 
         def sb(name, shape, dtype, after=None):
@@ -102,8 +101,7 @@ def tile_list_scatb_kernel(
         for cols in (EARLY, LATE):
             nc.sync.dma_start(out=wgo_sb[:, cols], in_=wgo[:, cols])
 
-        window_bytes = 4 * T
-        zeros = placed.tile([P, P], F32, name="zeros", offset=window_bytes - 2 * P)
+        zeros = sb("zeros", [P, P], F32)
         nc.gpsimd.memset(zeros[:], 0.0)
         nc.gpsimd.affine_select(
             out=eye[:],
@@ -114,9 +112,6 @@ def tile_list_scatb_kernel(
             pattern=[[-1, P]],
             channel_multiplier=1,
         )
-        for m in (2, 3):
-            win.append(placed.tile([P, T], F32, name="win%d" % m, offset=window_bytes * (m - 2)))
-            nc.gpsimd.memset(win[m][:].bitcast(I32), 0)
 
         nc.vector.memset(eye4[:].bitcast(I32), 0)
         nc.scalar.copy(
@@ -243,6 +238,9 @@ def tile_list_scatb_kernel(
             turn_back(0, pair, rts, r0, 2 + pair)
         for q in range(1, PACK):
             gather(g0, q, EVERY)
+        for m in (2, 3):
+            win.append(sb("win%d" % m, [P, T], F32, "x%d" % (m - 1)))
+            nc.gpsimd.memset(win[m][:].bitcast(I32), 0)
 
         g1 = sb("g1", [P, PACK * J], F32, "x0")
         gather(g1, 4, EVERY)
@@ -288,7 +286,7 @@ def tile_list_scatb_kernel(
         scatter(1, Q1, project("q11", 1, Q1, early_passes(Q1), 7))
 
         late_passes = ((WX, cq1, OWN), (0, xq0, LATE), (1, xq1_late, OWN), (WX, cr1, OWN))
-        for m, plane in enumerate(("x1", "x2", "x3", "x7")):
+        for m, plane in enumerate(("x3", "x5", "x6", "x7")):
             passes = late_passes[::-1] if m == 1 else late_passes
             scatter(m, LATE, project("late%d" % m, m, LATE, passes, 1 if m % 2 else 4, plane))
             rows = slice(m * P, (m + 1) * P)

@@ -22,6 +22,7 @@ BANK = 512
 GROUP = 16
 ROW_TILES = N // P
 WX = 2
+SQUARE = 32
 HALF = J // 2
 QUARTER = J // 4
 Q0, Q1, LATE = slice(0, QUARTER), slice(QUARTER, HALF), slice(HALF, J)
@@ -36,10 +37,14 @@ def tile_list_scatb_kernel(
     with ExitStack() as ctx:
         lists = ctx.enter_context(tc.tile_pool(name="lists", bufs=1))
         keep = ctx.enter_context(tc.tile_pool(name="keep", bufs=1))
+        placed = ctx.enter_context(tc.tile_pool(name="placed", bufs=1))
         psum = ctx.enter_context(tc.psum_pool(name="psum", bufs=1))
 
         def sb(name, shape, dtype, after=None):
             return keep.tile(shape, dtype, name=name, tag=after or name, align_bytes=64)
+
+        def at_offset(name, shape, dtype, offset):
+            return placed.tile(shape, dtype, name=name, offset=offset, align_bytes=64)
 
         def bank(name, n):
             return psum.tile([P, BANK], F32, name=name, tag="bank%d" % n)
@@ -55,24 +60,24 @@ def tile_list_scatb_kernel(
         x_sb = [sb("x%d" % q, [P, T], F32) for q in range(2 * PACK)]
         c_sb = [sb("c%d" % h, [P, PACK, HALF], F32) for h in range(2)]
         wgt_sb = sb("wgt", [P, J], F32)
+        wgt_in = sb("wgt_in", [P, 2, SQUARE], F32)
+        wgt_turned = sb("wgt_turned", [P, 2, SQUARE], F32)
+        wgt_rep = sb("wgt_rep", [P, J], F32)
         wgo_sb = sb("wgo", [P, J], F32)
         wt_w = sb("wt_w", [P, 2, N], U32)
         wx_w = sb("wx_w", [P, N], U32)
         bias = sb("bias", [P, ROW_TILES], F32)
         eye = sb("eye", [P, P], F32)
-        eye4 = sb("eye4", [P, PACK * (L + 1)], BF16)
+        eye4 = at_offset("eye4", [P, PACK * (L + 1)], BF16, 4096)
         eye_w = sb("eye_w", [P, L], U32)
         eye_s = sb("eye_s", [P, L], U8)
-        win = [sb("win%d" % m, [P, T], F32) for m in range(2)]
+        win = [sb("win0", [P, T], F32)]
 
         x_planes = xT.rearrange("(a p i) t -> a i p t", a=2, i=PACK)
         c_rows = c.rearrange("(p i) j -> p i j", i=PACK)
 
         def load_x(q):
             nc.sync.dma_start(out=x_sb[q][:], in_=x_planes[q // PACK, q % PACK])
-
-        def load_c(h):
-            nc.sync.dma_start(out=c_sb[h][:], in_=c_rows[:, :, h * HALF:(h + 1) * HALF])
 
         def load_words(tile, words):
             nc.sync.dma_start(out=tile.bitcast(I32), in_=words.rearrange("p n i -> p (n i)").bitcast(I32))
@@ -84,14 +89,17 @@ def tile_list_scatb_kernel(
                     in_=scales[:, 4 * q:4 * q + 4, :].rearrange("a r n -> r a n").bitcast(I32),
                 )
 
-        load_c(0)
+        wgt_runs = wgt.rearrange("(q h r) (i e) -> q r i h e", h=2, r=GROUP, e=SQUARE)
+        for q in range(P // SQUARE):
+            nc.sync.dma_start(out=wgt_in[q * SQUARE:(q + 1) * SQUARE, :, :], in_=wgt_runs[q, 0])
+        for cols in (Q0, Q1):
+            nc.sync.dma_start(out=c_sb[0][:, :, cols], in_=c_rows[:, :, cols])
         nc.sync.dma_start(offs_sb[:], offs)
-        nc.sync.dma_start(out=wgt_sb[:], in_=wgt)
         for q in range(6):
             load_x(q)
         with nc.allow_non_contiguous_dma(reason="one bias value to a partition and row tile"):
             nc.sync.dma_start(out=bias[:], in_=b.rearrange("(m p) -> p m", p=P))
-        load_c(1)
+        nc.sync.dma_start(out=c_sb[1][:], in_=c_rows[:, :, LATE])
         load_x(6)
         load_words(wx_w[:], wx_words[0])
         load_x(7)
@@ -101,7 +109,8 @@ def tile_list_scatb_kernel(
         for cols in (EARLY, LATE):
             nc.sync.dma_start(out=wgo_sb[:, cols], in_=wgo[:, cols])
 
-        zeros = sb("zeros", [P, P], F32)
+        zeros = at_offset("zeros", [P, P], F32, 0)
+        nc.gpsimd.memset(eye4[:].bitcast(I32), 0)
         nc.gpsimd.memset(zeros[:], 0.0)
         nc.gpsimd.affine_select(
             out=eye[:],
@@ -113,13 +122,18 @@ def tile_list_scatb_kernel(
             channel_multiplier=1,
         )
 
-        nc.vector.memset(eye4[:].bitcast(I32), 0)
         nc.scalar.copy(
             out=eye4[:].rearrange("p (t x) -> p t x", t=PACK)[:, :, 0:L:PACK],
             in_=eye[:].unsqueeze(1).to_broadcast([P, PACK, P]),
         )
-        for m in range(2):
-            nc.vector.memset(win[m][:].bitcast(I32), 0)
+        nc.vector.memset(win[0][:].bitcast(I32), 0)
+        for h in range(2):
+            nc.vector.transpose(wgt_turned[:, h, :], wgt_in[:, h, :])
+        nc.vector.tensor_copy(
+            out=wgt_rep[:].rearrange("p (i h r) -> p i h r", h=2, r=GROUP),
+            in_=wgt_turned[:].rearrange("p h i -> p i h").unsqueeze(3).to_broadcast([P, SQUARE, 2, GROUP]),
+        )
+        nc.vector.transpose(wgt_sb[:], wgt_rep[:])
         nc.vector.quantize_mx(out=eye_w[:].bitcast(FP8X4), scales=eye_s[:], in_=eye4[:, 0:PACK * L])
 
         def interleave_into(z, src):
@@ -222,14 +236,17 @@ def tile_list_scatb_kernel(
             nc.vector.tensor_tensor(win[m][:].indirect(offs2_sb[:, list_cols(cols)]), y[:], wgo_sb[:, cols], MULT)
 
         cq0 = operand("cq0", HALF)
-        quantise(cq0, EARLY, interleave("zc0", c_sb[0][:]))
+        zc0 = at_offset("zc0", [P, PACK * HALF], BF16, 0)
+        for cols in (Q0, Q1):
+            interleave_into(zc0[:, PACK * cols.start:PACK * cols.stop], c_sb[0][:, :, cols])
+        quantise(cq0, EARLY, zc0)
 
-        w_s = sb("w_s", [P, 3, N], U8, "zc0")
+        w_s = at_offset("w_s", [P, 3, N], U8, 0)
         nc.gpsimd.memset(w_s[:].rearrange("p a n -> p (a n)").bitcast(I32), 0)
         load_scales(w_s[:, WX:WX + 1, :], wx_scales)
         load_scales(w_s[:, 0:WX, :], wt_scales)
 
-        g0 = sb("g0", [P, PACK * J], F32)
+        g0 = at_offset("g0", [P, PACK * J], F32, 2048)
         gather(g0, 0, EVERY)
         nq = negated_values(0, cq0, (2, 3, 4, 5))
         rts = [turned_residual(0, s, nq, n) for s, n in enumerate((6, 7, 0, 1))]
@@ -238,11 +255,11 @@ def tile_list_scatb_kernel(
             turn_back(0, pair, rts, r0, 2 + pair)
         for q in range(1, PACK):
             gather(g0, q, EVERY)
-        for m in (2, 3):
+        for m in range(1, ROW_TILES):
             win.append(sb("win%d" % m, [P, T], F32, "x%d" % (m - 1)))
             nc.gpsimd.memset(win[m][:].bitcast(I32), 0)
 
-        g1 = sb("g1", [P, PACK * J], F32, "x0")
+        g1 = sb("g1", [P, PACK * J], F32)
         gather(g1, 4, EVERY)
         cr0 = operand("cr0", HALF, "x4")
         quantise(cr0, EARLY, r0)

@@ -27,6 +27,7 @@ HALF = J // 2
 QUARTER = J // 4
 Q0, Q1, LATE = slice(0, QUARTER), slice(QUARTER, HALF), slice(HALF, J)
 EARLY, EVERY = slice(0, HALF), slice(0, J)
+HEAD_AT, EYE4_AT, G0_AT = 0, 4096, 2048
 OWN = slice(0, HALF)
 
 
@@ -68,7 +69,7 @@ def tile_list_scatb_kernel(
         wx_w = sb("wx_w", [P, N], U32)
         bias = sb("bias", [P, ROW_TILES], F32)
         eye = sb("eye", [P, P], F32)
-        eye4 = at_offset("eye4", [P, PACK * (L + 1)], BF16, 4096)
+        eye4 = at_offset("eye4", [P, PACK * (L + 1)], BF16, EYE4_AT)
         eye_w = sb("eye_w", [P, L], U32)
         eye_s = sb("eye_s", [P, L], U8)
         win = [sb("win0", [P, T], F32)]
@@ -82,16 +83,16 @@ def tile_list_scatb_kernel(
         def load_words(tile, words):
             nc.sync.dma_start(out=tile.bitcast(I32), in_=words.rearrange("p n i -> p (n i)").bitcast(I32))
 
-        def load_scales(plane, scales):
-            for q in range(4):
+        def load_scales(dst, scales):
+            for quad in range(4):
                 nc.gpsimd.dma_start(
-                    out=plane[32 * q:32 * q + 4, :, :].bitcast(I32),
-                    in_=scales[:, 4 * q:4 * q + 4, :].rearrange("a r n -> r a n").bitcast(I32),
+                    out=dst[32 * quad:32 * quad + 4, :, :].bitcast(I32),
+                    in_=scales[:, 4 * quad:4 * quad + 4, :].rearrange("a r n -> r a n").bitcast(I32),
                 )
 
-        wgt_runs = wgt.rearrange("(q h r) (i e) -> q r i h e", h=2, r=GROUP, e=SQUARE)
-        for q in range(P // SQUARE):
-            nc.sync.dma_start(out=wgt_in[q * SQUARE:(q + 1) * SQUARE, :, :], in_=wgt_runs[q, 0])
+        wgt_runs = wgt.rearrange("(quad side row) (i e) -> quad row i side e", side=2, row=GROUP, e=SQUARE)
+        for quad in range(P // SQUARE):
+            nc.sync.dma_start(out=wgt_in[quad * SQUARE:(quad + 1) * SQUARE, :, :], in_=wgt_runs[quad, 0])
         for cols in (Q0, Q1):
             nc.sync.dma_start(out=c_sb[0][:, :, cols], in_=c_rows[:, :, cols])
         nc.sync.dma_start(offs_sb[:], offs)
@@ -101,15 +102,15 @@ def tile_list_scatb_kernel(
             nc.sync.dma_start(out=bias[:], in_=b.rearrange("(m p) -> p m", p=P))
         nc.sync.dma_start(out=c_sb[1][:], in_=c_rows[:, :, LATE])
         load_x(6)
-        load_words(wx_w[:], wx_words[0])
         load_x(7)
+        load_words(wx_w[:], wx_words[0])
         for a in range(2):
             load_words(wt_w[:, a, :], wt_words[a])
         nc.sync.dma_start(offs2_sb[:], offs2)
         for cols in (EARLY, LATE):
             nc.sync.dma_start(out=wgo_sb[:, cols], in_=wgo[:, cols])
 
-        zeros = at_offset("zeros", [P, P], F32, 0)
+        zeros = at_offset("zeros", [P, P], F32, HEAD_AT)
         nc.gpsimd.memset(eye4[:].bitcast(I32), 0)
         nc.gpsimd.memset(zeros[:], 0.0)
         nc.gpsimd.affine_select(
@@ -126,12 +127,13 @@ def tile_list_scatb_kernel(
             out=eye4[:].rearrange("p (t x) -> p t x", t=PACK)[:, :, 0:L:PACK],
             in_=eye[:].unsqueeze(1).to_broadcast([P, PACK, P]),
         )
+
         nc.vector.memset(win[0][:].bitcast(I32), 0)
-        for h in range(2):
-            nc.vector.transpose(wgt_turned[:, h, :], wgt_in[:, h, :])
+        for side in range(2):
+            nc.vector.transpose(wgt_turned[:, side, :], wgt_in[:, side, :])
         nc.vector.tensor_copy(
-            out=wgt_rep[:].rearrange("p (i h r) -> p i h r", h=2, r=GROUP),
-            in_=wgt_turned[:].rearrange("p h i -> p i h").unsqueeze(3).to_broadcast([P, SQUARE, 2, GROUP]),
+            out=wgt_rep[:].rearrange("p (i side row) -> p i side row", side=2, row=GROUP),
+            in_=wgt_turned[:].rearrange("p side i -> p i side").unsqueeze(3).to_broadcast([P, SQUARE, 2, GROUP]),
         )
         nc.vector.transpose(wgt_sb[:], wgt_rep[:])
         nc.vector.quantize_mx(out=eye_w[:].bitcast(FP8X4), scales=eye_s[:], in_=eye4[:, 0:PACK * L])
@@ -236,17 +238,17 @@ def tile_list_scatb_kernel(
             nc.vector.tensor_tensor(win[m][:].indirect(offs2_sb[:, list_cols(cols)]), y[:], wgo_sb[:, cols], MULT)
 
         cq0 = operand("cq0", HALF)
-        zc0 = at_offset("zc0", [P, PACK * HALF], BF16, 0)
+        zc0 = at_offset("zc0", [P, PACK * HALF], BF16, HEAD_AT)
         for cols in (Q0, Q1):
             interleave_into(zc0[:, PACK * cols.start:PACK * cols.stop], c_sb[0][:, :, cols])
         quantise(cq0, EARLY, zc0)
 
-        w_s = at_offset("w_s", [P, 3, N], U8, 0)
+        w_s = at_offset("w_s", [P, 3, N], U8, HEAD_AT)
         nc.gpsimd.memset(w_s[:].rearrange("p a n -> p (a n)").bitcast(I32), 0)
         load_scales(w_s[:, WX:WX + 1, :], wx_scales)
         load_scales(w_s[:, 0:WX, :], wt_scales)
 
-        g0 = at_offset("g0", [P, PACK * J], F32, 2048)
+        g0 = at_offset("g0", [P, PACK * J], F32, G0_AT)
         gather(g0, 0, EVERY)
         nq = negated_values(0, cq0, (2, 3, 4, 5))
         rts = [turned_residual(0, s, nq, n) for s, n in enumerate((6, 7, 0, 1))]
@@ -255,6 +257,7 @@ def tile_list_scatb_kernel(
             turn_back(0, pair, rts, r0, 2 + pair)
         for q in range(1, PACK):
             gather(g0, q, EVERY)
+
         for m in range(1, ROW_TILES):
             win.append(sb("win%d" % m, [P, T], F32, "x%d" % (m - 1)))
             nc.gpsimd.memset(win[m][:].bitcast(I32), 0)

@@ -68,6 +68,7 @@ def tile_list_scatb_kernel(
         wt_w = sb("wt_w", [P, 2, N], U32)
         wx_w = sb("wx_w", [P, N], U32)
         bias = sb("bias", [P, ROW_TILES], F32)
+        bias_q0 = sb("bias_q0", [P, 2], F32)
         eye = sb("eye", [P, P], F32)
         eye4 = at_offset("eye4", [P, PACK * (L + 1)], BF16, EYE4_AT)
         eye_w = sb("eye_w", [P, L], U32)
@@ -86,8 +87,8 @@ def tile_list_scatb_kernel(
         def load_scales(dst, scales):
             for quad in range(4):
                 nc.gpsimd.dma_start(
-                    out=dst[32 * quad:32 * quad + 4, :, :].bitcast(I32),
-                    in_=scales[:, 4 * quad:4 * quad + 4, :].rearrange("a r n -> r a n").bitcast(I32),
+                    out=dst[32 * quad:32 * quad + 4 * scales.shape[0], :].bitcast(I32),
+                    in_=scales[:, 4 * quad:4 * quad + 4, :].bitcast(I32),
                 )
 
         wgt_runs = wgt.rearrange("(quad side row) (i e) -> quad row i side e", side=2, row=GROUP, e=SQUARE)
@@ -98,17 +99,19 @@ def tile_list_scatb_kernel(
         nc.sync.dma_start(offs_sb[:], offs)
         for q in range(6):
             load_x(q)
-        with nc.allow_non_contiguous_dma(reason="one bias value to a partition and row tile"):
-            nc.sync.dma_start(out=bias[:], in_=b.rearrange("(m p) -> p m", p=P))
         nc.sync.dma_start(out=c_sb[1][:], in_=c_rows[:, :, LATE])
         load_x(6)
         load_x(7)
         load_words(wx_w[:], wx_words[0])
         for a in range(2):
             load_words(wt_w[:, a, :], wt_words[a])
-        nc.sync.dma_start(offs2_sb[:], offs2)
-        for cols in (EARLY, LATE):
-            nc.sync.dma_start(out=wgo_sb[:, cols], in_=wgo[:, cols])
+        b_cols = b.rearrange("(m p) -> p m", p=P)
+        with nc.allow_non_contiguous_dma(reason="one bias value to a partition and row tile"):
+            nc.sync.dma_start(out=bias_q0[:], in_=b_cols[:, 0:2])
+            nc.sync.dma_start(offs2_sb[:], offs2)
+            nc.sync.dma_start(out=wgo_sb[:, EARLY], in_=wgo[:, EARLY])
+            nc.sync.dma_start(out=bias[:], in_=b_cols)
+        nc.sync.dma_start(out=wgo_sb[:, LATE], in_=wgo[:, LATE])
 
         zeros = at_offset("zeros", [P, P], F32, HEAD_AT)
         nc.gpsimd.memset(eye4[:].bitcast(I32), 0)
@@ -224,7 +227,7 @@ def tile_list_scatb_kernel(
                 nc.tensor.matmul_mx(
                     out=acc,
                     lhsT=words.bitcast(FP8X4),
-                    lhsT_scale=w_s[:, a, rows],
+                    lhsT_scale=w_s[:, 0, rows] if a == WX else w_s[4 * a:P, 1, rows],
                     rhs=op[0][:, at].bitcast(FP8X4),
                     rhs_scale=op[1][:, at],
                     start=(i == 0),
@@ -243,10 +246,10 @@ def tile_list_scatb_kernel(
             interleave_into(zc0[:, PACK * cols.start:PACK * cols.stop], c_sb[0][:, :, cols])
         quantise(cq0, EARLY, zc0)
 
-        w_s = at_offset("w_s", [P, 3, N], U8, HEAD_AT)
+        w_s = at_offset("w_s", [P, 2, N], U8, HEAD_AT)
         nc.gpsimd.memset(w_s[:].rearrange("p a n -> p (a n)").bitcast(I32), 0)
-        load_scales(w_s[:, WX:WX + 1, :], wx_scales)
-        load_scales(w_s[:, 0:WX, :], wt_scales)
+        load_scales(w_s[:, 0, :], wx_scales)
+        load_scales(w_s[:, 1, :], wt_scales)
 
         g0 = at_offset("g0", [P, PACK * J], F32, G0_AT)
         gather(g0, 0, EVERY)
@@ -274,8 +277,6 @@ def tile_list_scatb_kernel(
         quantise(xq0, EVERY, z0)
         gather(g1, 6, EVERY)
         zc1 = interleave("zc1", c_sb[1][:])
-        bias_q0 = sb("bias_q0", [P, 2], F32)
-        nc.scalar.copy(out=bias_q0[:], in_=bias[:, 0:2])
         for cols in (Q0, Q1, LATE):
             gather(g1, 7, cols)
 

@@ -91,9 +91,8 @@ def tile_list_scatb_kernel(
                     in_=scales[:, 4 * quad:4 * quad + 4, :].bitcast(I32),
                 )
 
-        wgt_runs = wgt.rearrange("(quad side row) (i e) -> quad row i side e", side=2, row=GROUP, e=SQUARE)
-        for quad in range(P // SQUARE):
-            nc.sync.dma_start(out=wgt_in[quad * SQUARE:(quad + 1) * SQUARE, :, :], in_=wgt_runs[quad, 0])
+        wgt_rows = wgt.rearrange("(g row) (i x) -> row g i x", row=GROUP, i=GROUP)
+        nc.sync.dma_start(out=wgt_in[:].rearrange("p h e -> p (h e)"), in_=wgt_rows[0])
         for cols in (Q0, Q1):
             nc.sync.dma_start(out=c_sb[0][:, :, cols], in_=c_rows[:, :, cols])
         nc.sync.dma_start(offs_sb[:], offs)
@@ -132,11 +131,11 @@ def tile_list_scatb_kernel(
         )
 
         nc.vector.memset(win[0][:].bitcast(I32), 0)
-        for side in range(2):
-            nc.vector.transpose(wgt_turned[:, side, :], wgt_in[:, side, :])
+        for h in range(2):
+            nc.vector.transpose(wgt_turned[:, h, :], wgt_in[:, h, :])
         nc.vector.tensor_copy(
-            out=wgt_rep[:].rearrange("p (i side row) -> p i side row", side=2, row=GROUP),
-            in_=wgt_turned[:].rearrange("p side i -> p i side").unsqueeze(3).to_broadcast([P, SQUARE, 2, GROUP]),
+            out=wgt_rep[:].rearrange("p (i hs row) -> p i hs row", hs=4, row=GROUP),
+            in_=wgt_turned[:].rearrange("p h (side i) -> p i (h side)", side=2).unsqueeze(3).to_broadcast([P, GROUP, 4, GROUP]),
         )
         nc.vector.transpose(wgt_sb[:], wgt_rep[:])
         nc.vector.quantize_mx(out=eye_w[:].bitcast(FP8X4), scales=eye_s[:], in_=eye4[:, 0:PACK * L])

@@ -28,6 +28,7 @@ QUARTER = J // 4
 Q0, Q1, LATE = slice(0, QUARTER), slice(QUARTER, HALF), slice(HALF, J)
 EARLY, EVERY = slice(0, HALF), slice(0, J)
 HEAD_AT, EYE4_AT, G0_AT = 0, 4096, 2048
+SHARE = 208
 OWN = slice(0, HALF)
 
 
@@ -63,7 +64,7 @@ def tile_list_scatb_kernel(
         wgt_sb = sb("wgt", [P, J], F32)
         wgt_in = sb("wgt_in", [P, 2, SQUARE], F32)
         wgt_turned = sb("wgt_turned", [P, 2, SQUARE], F32)
-        wgt_rep = sb("wgt_rep", [P, J], F32)
+        wgt_rep = at_offset("wgt_rep", [P, J], F32, HEAD_AT)
         wgo_sb = sb("wgo", [P, J], F32)
         wt_w = sb("wt_w", [P, 2, N], U32)
         wx_w = sb("wx_w", [P, N], U32)
@@ -93,8 +94,7 @@ def tile_list_scatb_kernel(
 
         wgt_rows = wgt.rearrange("(g row) (i x) -> row g i x", row=GROUP, i=GROUP)
         nc.sync.dma_start(out=wgt_in[:].rearrange("p h e -> p (h e)"), in_=wgt_rows[0])
-        for cols in (Q0, Q1):
-            nc.sync.dma_start(out=c_sb[0][:, :, cols], in_=c_rows[:, :, cols])
+        nc.sync.dma_start(out=c_sb[0][:], in_=c_rows[:, :, EARLY])
         nc.sync.dma_start(offs_sb[:], offs)
         for q in range(6):
             load_x(q)
@@ -133,15 +133,18 @@ def tile_list_scatb_kernel(
         nc.vector.memset(win[0][:].bitcast(I32), 0)
         for h in range(2):
             nc.vector.transpose(wgt_turned[:, h, :], wgt_in[:, h, :])
-        nc.vector.tensor_copy(
-            out=wgt_rep[:].rearrange("p (i hs row) -> p i hs row", hs=4, row=GROUP),
-            in_=wgt_turned[:].rearrange("p h (side i) -> p i (h side)", side=2).unsqueeze(3).to_broadcast([P, GROUP, 4, GROUP]),
-        )
-        nc.vector.transpose(wgt_sb[:], wgt_rep[:])
+        runs = wgt_turned[:].rearrange("p h (side i) -> p i (h side)", side=2)
+        for half, cols in enumerate((EARLY, LATE)):
+            nc.vector.tensor_copy(
+                out=wgt_rep[:, cols].rearrange("p (i hs row) -> p i hs row", hs=4, row=GROUP),
+                in_=runs[:, 8 * half:8 * half + 8, :].unsqueeze(3).to_broadcast([P, 8, 4, GROUP]),
+            )
+        for cols in (EARLY, LATE):
+            nc.vector.transpose(wgt_sb[:, cols], wgt_rep[:, cols])
         nc.vector.quantize_mx(out=eye_w[:].bitcast(FP8X4), scales=eye_s[:], in_=eye4[:, 0:PACK * L])
 
-        def interleave_into(z, src):
-            nc.scalar.copy(
+        def interleave_into(z, src, copy=nc.scalar.copy):
+            copy(
                 out=z.rearrange("p (g e t) -> p g t e", e=4, t=PACK),
                 in_=src.rearrange("p t (g e) -> p g t e", e=4),
             )
@@ -241,8 +244,8 @@ def tile_list_scatb_kernel(
 
         cq0 = operand("cq0", HALF)
         zc0 = at_offset("zc0", [P, PACK * HALF], BF16, HEAD_AT)
-        for cols in (Q0, Q1):
-            interleave_into(zc0[:, PACK * cols.start:PACK * cols.stop], c_sb[0][:, :, cols])
+        for cols, copy in ((slice(0, SHARE), nc.scalar.copy), (slice(SHARE, HALF), nc.vector.tensor_copy)):
+            interleave_into(zc0[:, PACK * cols.start:PACK * cols.stop], c_sb[0][:, :, cols], copy)
         quantise(cq0, EARLY, zc0)
 
         w_s = at_offset("w_s", [P, 2, N], U8, HEAD_AT)

@@ -145,8 +145,8 @@ def tile_list_scatb_kernel(
 
         def interleave_into(z, src, copy=nc.scalar.copy):
             copy(
-                out=z.rearrange("p (g e t) -> p g t e", e=4, t=PACK),
-                in_=src.rearrange("p t (g e) -> p g t e", e=4),
+                out=z.rearrange("p (g e t) -> p g t e", e=2, t=PACK),
+                in_=src.rearrange("p t (g e) -> p g t e", e=2),
             )
 
         def interleave(name, src, after=None):

from contextlib import ExitStack

import concourse.mybir as mybir

K, L, N, T, J = 1024, 512, 512, 2048, 1024
FLOPS = 2 * (K + 2 * L) * N * J + 2 * L * L * J

F32 = mybir.dt.float32
BF16 = mybir.dt.bfloat16
I32 = mybir.dt.int32
U32 = mybir.dt.uint32
U16 = mybir.dt.uint16
U8 = mybir.dt.uint8
FP8X4 = mybir.dt.float8_e4m3fn_x4
MULT = mybir.AluOpType.mult
IDENT = mybir.ActivationFunctionType.Identity
COPY = mybir.ActivationFunctionType.Copy

P = 128
PACK = 4
BANK = 512
GROUP = 16
ROW_TILES = N // P
WX = 2
SQUARE = 32
HALF = J // 2
QUARTER = J // 4
Q0, Q1, LATE = slice(0, QUARTER), slice(QUARTER, HALF), slice(HALF, J)
EARLY, EVERY = slice(0, HALF), slice(0, J)
HEAD_AT, EYE4_AT, G0_AT = 0, 4096, 2048
SHARE = 208
OWN = slice(0, HALF)


def tile_list_scatb_kernel(
    tc, xT, wgt, wt_words, wt_scales, c, wx_words, wx_scales, b, wgo, offs, offs2, out
):
    nc = tc.nc
    with ExitStack() as ctx:
        lists = ctx.enter_context(tc.tile_pool(name="lists", bufs=1))
        keep = ctx.enter_context(tc.tile_pool(name="keep", bufs=1))
        placed = ctx.enter_context(tc.tile_pool(name="placed", bufs=1))
        psum = ctx.enter_context(tc.psum_pool(name="psum", bufs=1))

        def sb(name, shape, dtype, after=None):
            return keep.tile(shape, dtype, name=name, tag=after or name, align_bytes=64)

        def at_offset(name, shape, dtype, offset):
            return placed.tile(shape, dtype, name=name, offset=offset, align_bytes=64)

        def bank(name, n):
            return psum.tile([P, BANK], F32, name=name, tag="bank%d" % n)

        def width(cols):
            return cols.stop - cols.start

        def list_cols(cols):
            return slice(cols.start // GROUP, cols.stop // GROUP)

        offs_sb = lists.tile([P, J // GROUP], U16, name="offs_sb")
        offs2_sb = lists.tile([P, J // GROUP], U16, name="offs2_sb")
        x_sb = [sb("x%d" % q, [P, T], F32) for q in range(2 * PACK)]
        c_sb = [sb("c%d" % h, [P, PACK, HALF], F32) for h in range(2)]
        wgt_sb = sb("wgt", [P, J], F32)
        wgt_in = sb("wgt_in", [P, 2, SQUARE], F32)
        wgt_turned = sb("wgt_turned", [P, 2, SQUARE], F32)
        wgt_rep = at_offset("wgt_rep", [P, J], F32, HEAD_AT)
        wgo_sb = sb("wgo", [P, J], F32)
        wt_w = sb("wt_w", [P, 2, N], U32)
        wx_w = sb("wx_w", [P, N], U32)
        bias = sb("bias", [P, ROW_TILES], F32)
        bias_q0 = sb("bias_q0", [P, 2], F32)
        eye = sb("eye", [P, P], F32)
        eye4 = at_offset("eye4", [P, PACK * (L + 1)], BF16, EYE4_AT)
        eye_w = sb("eye_w", [P, L], U32)
        eye_s = sb("eye_s", [P, L], U8)
        win = [sb("win0", [P, T], F32)]

        x_planes = xT.rearrange("(a p i) t -> a i p t", a=2, i=PACK)
        c_rows = c.rearrange("(p i) j -> p i j", i=PACK)

        def load_x(q):
            nc.sync.dma_start(out=x_sb[q][:], in_=x_planes[q // PACK, q % PACK])

        def load_words(tile, words):
            nc.sync.dma_start(out=tile.bitcast(I32), in_=words.rearrange("p n i -> p (n i)").bitcast(I32))

        def load_scales(dst, scales):
            for quad in range(4):
                nc.gpsimd.dma_start(
                    out=dst[32 * quad:32 * quad + 4 * scales.shape[0], :].bitcast(I32),
                    in_=scales[:, 4 * quad:4 * quad + 4, :].bitcast(I32),
                )

        wgt_rows = wgt.rearrange("(g row) (i x) -> row g i x", row=GROUP, i=GROUP)
        nc.sync.dma_start(out=wgt_in[:].rearrange("p h e -> p (h e)"), in_=wgt_rows[0])
        nc.sync.dma_start(out=c_sb[0][:], in_=c_rows[:, :, EARLY])
        nc.sync.dma_start(offs_sb[:], offs)
        for q in range(6):
            load_x(q)
        nc.sync.dma_start(out=c_sb[1][:], in_=c_rows[:, :, LATE])
        load_x(6)
        load_x(7)
        load_words(wx_w[:], wx_words[0])
        for a in range(2):
            load_words(wt_w[:, a, :], wt_words[a])
        b_cols = b.rearrange("(m p) -> p m", p=P)
        with nc.allow_non_contiguous_dma(reason="one bias value to a partition and row tile"):
            nc.sync.dma_start(out=bias_q0[:], in_=b_cols[:, 0:2])
            nc.sync.dma_start(offs2_sb[:], offs2)
            nc.sync.dma_start(out=wgo_sb[:, EARLY], in_=wgo[:, EARLY])
            nc.sync.dma_start(out=bias[:], in_=b_cols)
        nc.sync.dma_start(out=wgo_sb[:, LATE], in_=wgo[:, LATE])

        zeros = at_offset("zeros", [P, P], F32, HEAD_AT)
        nc.gpsimd.memset(eye4[:].bitcast(I32), 0)
        nc.gpsimd.memset(zeros[:], 0.0)
        nc.gpsimd.affine_select(
            out=eye[:],
            in_=zeros[:],
            compare_op=mybir.AluOpType.not_equal,
            fill=1.0,
            base=0,
            pattern=[[-1, P]],
            channel_multiplier=1,
        )

        nc.scalar.copy(
            out=eye4[:].rearrange("p (t x) -> p t x", t=PACK)[:, :, 0:L:PACK],
            in_=eye[:].unsqueeze(1).to_broadcast([P, PACK, P]),
        )

        nc.vector.memset(win[0][:].bitcast(I32), 0)
        for h in range(2):
            nc.vector.transpose(wgt_turned[:, h, :], wgt_in[:, h, :])
        runs = wgt_turned[:].rearrange("p h (side i) -> p i (h side)", side=2)
        for half, cols in enumerate((EARLY, LATE)):
            nc.vector.tensor_copy(
                out=wgt_rep[:, cols].rearrange("p (i hs row) -> p i hs row", hs=4, row=GROUP),
                in_=runs[:, 8 * half:8 * half + 8, :].unsqueeze(3).to_broadcast([P, 8, 4, GROUP]),
            )
        for cols in (EARLY, LATE):
            nc.vector.transpose(wgt_sb[:, cols], wgt_rep[:, cols])
        nc.vector.quantize_mx(out=eye_w[:].bitcast(FP8X4), scales=eye_s[:], in_=eye4[:, 0:PACK * L])

        def interleave_into(z, src, copy=nc.scalar.copy):
            copy(
                out=z.rearrange("p (g e t) -> p g t e", e=2, t=PACK),
                in_=src.rearrange("p t (g e) -> p g t e", e=2),
            )

        def interleave(name, src, after=None):
            z = sb(name, [P, PACK * src.shape[2]], BF16, after)
            interleave_into(z[:], src)
            return z

        def operand(name, cols, after=None):
            return sb(name + "_w", [P, cols], U32, after), sb(name + "_s", [P, cols], U8)

        def quantise(op, cols, z):
            nc.vector.quantize_mx(out=op[0][:, cols].bitcast(FP8X4), scales=op[1][:, cols], in_=z[:])

        def negated_values(h, cq, banks):
            nq = sb("nq%d" % h, [P, PACK, HALF], F32, "nq")
            for t in range(PACK):
                dq = bank("dq%d%d" % (h, t), banks[t])
                nc.tensor.matmul_mx(
                    out=dq[:],
                    lhsT=eye_w[:, t * P:(t + 1) * P].bitcast(FP8X4),
                    lhsT_scale=eye_s[:, t * P:(t + 1) * P],
                    rhs=cq[0][:].bitcast(FP8X4),
                    rhs_scale=cq[1][:],
                    start=True,
                    stop=True,
                )
                nc.scalar.activation(out=nq[:, t, :], in_=dq[:], func=COPY, scale=-1.0)
            return nq

        def turned_residual(h, s, nq, n):
            cols = slice(s * P, (s + 1) * P)
            diff = bank("diff%d%d" % (h, s), n)
            for term, src in enumerate((c_sb[h], nq)):
                for t in range(PACK):
                    nc.tensor.matmul(
                        diff[:, t * P:(t + 1) * P],
                        lhsT=src[:, t, cols],
                        rhs=eye[:],
                        start=(term == 0 and t == 0),
                        stop=(term == 1 and t == PACK - 1),
                        is_transpose=True,
                    )
            rt = sb("rt%d%d" % (h, s), [P, L], BF16, "rt%d" % s)
            nc.scalar.copy(
                out=rt[:].rearrange("j (u g i e) -> j u g e i", u=2, i=2, e=2),
                in_=diff[:].rearrange("j (u e g i) -> j u g e i", u=2, e=2, i=2),
            )
            return rt

        def turn_back(h, pair, rts, r, n):
            back = bank("back%d%d" % (h, pair), n)
            for s in range(2):
                words = rts[2 * pair + s][:].bitcast(F32)
                for u in range(2):
                    at = (2 * s + u) * P
                    nc.tensor.transpose(back[:, at:at + P], words[:, u * P:(u + 1) * P], eye[:])
            r_words = r[:].bitcast(F32)[:, pair * BANK:(pair + 1) * BANK]
            nc.scalar.copy(
                out=r_words.rearrange("p (s g i u) -> p s g u i", s=2, i=2, u=2),
                in_=back[:].rearrange("p (s u g i) -> p s g u i", s=2, u=2, i=2),
            )

        def gather(g, q, cols):
            at = (q % PACK) * J
            nc.vector.tensor_tensor(
                g[:, at + cols.start:at + cols.stop],
                x_sb[q][:].indirect(offs_sb[:, list_cols(cols)]),
                wgt_sb[:, cols],
                MULT,
            )

        def planes(g, cols):
            return g[:].rearrange("p (t j) -> p t j", t=PACK)[:, :, cols]

        def project(name, m, cols, passes, n, after=None, shift=bias):
            acc = bank("acc" + name, n)[:, 0:width(cols)]
            rows = slice(m * P, (m + 1) * P)
            for i, (a, op, at) in enumerate(passes):
                words = wx_w[:, rows] if a == WX else wt_w[:, a, rows]
                nc.tensor.matmul_mx(
                    out=acc,
                    lhsT=words.bitcast(FP8X4),
                    lhsT_scale=w_s[:, 0, rows] if a == WX else w_s[4 * a:P, 1, rows],
                    rhs=op[0][:, at].bitcast(FP8X4),
                    rhs_scale=op[1][:, at],
                    start=(i == 0),
                    stop=(i == len(passes) - 1),
                )
            y = sb("y" + name, [P, width(cols)], F32, after)
            nc.scalar.activation(out=y[:], in_=acc, func=IDENT, bias=shift[:, m:m + 1])
            return y

        def scatter(m, cols, y):
            nc.vector.tensor_tensor(win[m][:].indirect(offs2_sb[:, list_cols(cols)]), y[:], wgo_sb[:, cols], MULT)

        cq0 = operand("cq0", HALF)
        zc0 = at_offset("zc0", [P, PACK * HALF], BF16, HEAD_AT)
        for cols, copy in ((slice(0, SHARE), nc.scalar.copy), (slice(SHARE, HALF), nc.vector.tensor_copy)):
            interleave_into(zc0[:, PACK * cols.start:PACK * cols.stop], c_sb[0][:, :, cols], copy)
        quantise(cq0, EARLY, zc0)

        w_s = at_offset("w_s", [P, 2, N], U8, HEAD_AT)
        nc.gpsimd.memset(w_s[:].rearrange("p a n -> p (a n)").bitcast(I32), 0)
        load_scales(w_s[:, 0, :], wx_scales)
        load_scales(w_s[:, 1, :], wt_scales)

        g0 = at_offset("g0", [P, PACK * J], F32, G0_AT)
        gather(g0, 0, EVERY)
        nq = negated_values(0, cq0, (2, 3, 4, 5))
        rts = [turned_residual(0, s, nq, n) for s, n in enumerate((6, 7, 0, 1))]
        r0 = sb("r0", [P, PACK * HALF], BF16)
        for pair in range(2):
            turn_back(0, pair, rts, r0, 2 + pair)
        for q in range(1, PACK):
            gather(g0, q, EVERY)

        for m in range(1, ROW_TILES):
            win.append(sb("win%d" % m, [P, T], F32, "x%d" % (m - 1)))
            nc.gpsimd.memset(win[m][:].bitcast(I32), 0)

        g1 = sb("g1", [P, PACK * J], F32)
        gather(g1, 4, EVERY)
        cr0 = operand("cr0", HALF, "x4")
        quantise(cr0, EARLY, r0)
        z0 = sb("z0", [P, PACK * J], BF16)
        for cols in (EARLY, LATE):
            interleave_into(z0[:, PACK * cols.start:PACK * cols.stop], planes(g0, cols))
        gather(g1, 5, EVERY)
        xq0 = operand("xq0", J)
        quantise(xq0, EVERY, z0)
        gather(g1, 6, EVERY)
        zc1 = interleave("zc1", c_sb[1][:])
        for cols in (Q0, Q1, LATE):
            gather(g1, 7, cols)

        xq1 = operand("xq1", HALF)
        quantise(xq1, Q0, interleave("z1q0", planes(g1, Q0)))
        cq1 = operand("cq1", HALF, "z1q0")
        quantise(cq1, OWN, zc1)
        quantise(xq1, Q1, interleave("z1q1", planes(g1, Q1)))

        def early_passes(cols):
            return ((WX, cq0, cols), (WX, cr0, cols), (0, xq0, cols), (1, xq1, cols))

        for m in (0, 1):
            scatter(m, Q0, project("q0%d" % m, m, Q0, early_passes(Q0), m, None, bias_q0))
        xq1_late = operand("xq1_late", HALF)
        quantise(xq1_late, OWN, interleave("z1_late", planes(g1, LATE), "bias_q0"))
        for m in (2, 3):
            scatter(m, EARLY, project("early%d" % m, m, EARLY, early_passes(EARLY), m))

        nq = negated_values(1, cq1, range(PACK))
        rts = [turned_residual(1, s, nq, PACK + s) for s in range(PACK)]
        scatter(0, Q1, project("q10", 0, Q1, early_passes(Q1), 3))
        r1 = sb("r1", [P, PACK * HALF], BF16, "r0")
        for pair in range(2):
            turn_back(1, pair, rts, r1, pair)
        cr1 = operand("cr1", HALF)
        quantise(cr1, OWN, r1)
        scatter(1, Q1, project("q11", 1, Q1, early_passes(Q1), 7))

        late_passes = ((WX, cq1, OWN), (0, xq0, LATE), (1, xq1_late, OWN), (WX, cr1, OWN))
        for m, plane in enumerate(("x3", "x5", "x6", "x7")):
            passes = late_passes[::-1] if m == 1 else late_passes
            scatter(m, LATE, project("late%d" % m, m, LATE, passes, 1 if m % 2 else 4, plane))
            rows = slice(m * P, (m + 1) * P)
            if m < ROW_TILES - 1:
                nc.sync.dma_start(out=out[rows, :], in_=win[m][:])
            else:
                nc.sync.dma_start(out=out[rows, 0:T // 2], in_=win[m][:, 0:T // 2])
                nc.scalar.dma_start(out=out[rows, T // 2:T], in_=win[m][:, T // 2:T])
